import numpy as np
import ml_dtypes


def mxq(x, axis, fmt="e4m3"):
    dtype, down = {"e4m3": (ml_dtypes.float8_e4m3fn, 7), "e5m2": (ml_dtypes.float8_e5m2, 14)}[fmt]
    v = np.moveaxis(np.asarray(x, np.float32).astype(ml_dtypes.bfloat16).astype(np.float64), axis, -1)
    blocks = v.reshape(v.shape[:-1] + (-1, 32))
    amax = np.abs(blocks).max(-1, keepdims=True)
    byte = np.maximum(np.where(amax > 0, np.frexp(amax)[1] - 1 + 127, 0) - down, 1)
    scale = np.exp2(byte - 127.0)
    codes = (blocks / scale).astype(np.float32).astype(dtype).astype(np.float64)
    return np.moveaxis((codes * scale).reshape(v.shape), -1, axis)


WIDE = False


def mx_kscale(k):
    if not WIDE:
        return np.ones(k)
    levels = np.array([10, -10, 5, -5, 0])
    if k % 512:
        return np.exp2(np.random.permutation(np.resize(levels, k // 32))).repeat(32)
    a = np.empty((k // 512, 16))
    for p in range(k // 512):
        a[p, :8] = np.random.permutation(np.resize(levels, 8))
        for g in range(8):
            far = levels[np.abs(levels - a[p, g]) >= 10]
            a[p, g + 8] = far[np.random.randint(len(far))]
    return np.exp2(a.ravel()).repeat(32)


def f64(x):
    return np.asarray(x).astype(np.float64)


def striped(idx):
    return np.tile(idx.reshape(-1, 16).T, (8, 1)).astype(np.uint16)


def unstriped(offs):
    return offs[:16].T.reshape(-1).astype(np.int64)


E2M1 = np.array([0.0, 0.5, 1.0, 1.5, 2.0, 3.0, 4.0, 6.0, -0.0, -0.5, -1.0, -1.5, -2.0, -3.0, -4.0, -6.0])


def pack_weight(w, fmt):
    k, n = w.shape
    w = f64(np.asarray(w, np.float32).astype(ml_dtypes.bfloat16)).reshape(k // 32, 32, n)
    amax = np.abs(w).max(1)
    if fmt == "e4m3":
        byte = np.frexp(amax)[1] - 1 + 127 - 7
    else:
        mant, ex = np.frexp(amax / 6.0)
        byte = np.where(mant > 0.5, ex, ex - 1) + 127
    byte = np.clip(np.where(amax > 0, byte, 1), 1, 254)
    scaled = (w * np.exp2(127.0 - byte)[:, None, :]).reshape(k, n).astype(np.float32)
    by_word = np.ascontiguousarray(scaled.reshape(k // 512, 128, 4, n).transpose(0, 1, 3, 2))
    if fmt == "e4m3":
        words = by_word.astype(ml_dtypes.float8_e4m3fn).view(np.uint8)
    else:
        c = by_word.astype(ml_dtypes.float4_e2m1fn).view(np.uint8) & 0xF
        words = (c[..., 0::2] | (c[..., 1::2] << 4)).reshape(k // 512, 128, 2 * n)
    return np.ascontiguousarray(words), np.ascontiguousarray(byte.astype(np.uint8).reshape(k // 512, 16, n))


def unpack_weight(words, scales, fmt):
    g, _, n = scales.shape
    words = np.ascontiguousarray(words).reshape(g, 128, n, -1)
    if fmt == "e4m3":
        vals = words.view(ml_dtypes.float8_e4m3fn).astype(np.float64)
    else:
        nib = np.empty((g, 128, n, 4), np.uint8)
        nib[..., 0::2] = words & 0xF
        nib[..., 1::2] = words >> 4
        vals = E2M1[nib]
    vals = vals * np.repeat(np.exp2(scales.astype(np.float64) - 127.0), 8, axis=1)[..., None]
    return vals.transpose(0, 1, 3, 2).reshape(g * 512, n)


def gelu(v):
    return 0.5 * v * (1.0 + np.tanh(np.sqrt(2.0 / np.pi) * (v + 0.044715 * v**3)))


K, H, T, S, P = 1536, 1024, 2048, 1024, 512

def setup_inputs():
    n = np.random.standard_normal
    s = mx_kscale(K)[:, None]
    u = mx_kscale(H)[:, None]
    tab_words, tab_scales = pack_weight(n((K, T)) * s, "e4m3")
    w1 = n((K, H)) / np.sqrt(K) / s
    w4_words, w4_scales = pack_weight(1.5 * n((H, H)) / np.sqrt(H) / u, "e2m1")
    gain = 0.5 * np.exp(0.2 * n(H)) * u[:, 0]
    b = 0.4 * n(H) * u[:, 0]
    return {
        "tab_words": tab_words, "tab_scales": tab_scales,
        "offs": striped(np.random.permutation(T)[:S]),
        "w1": w1.astype(np.float32),
        "pos1": striped(np.random.permutation(S)[:P]),
        "gain": gain.astype(np.float32),
        "b": b.astype(np.float32),
        "w4_words": w4_words, "w4_scales": w4_scales,
        "pos2": striped(np.random.permutation(S)[:P]),
    }

def reference(tab_words, tab_scales, offs, w1, pos1, gain, b, w4_words, w4_scales, pos2):
    v = unpack_weight(tab_words, tab_scales, "e4m3")[:, unstriped(offs)]
    h = mxq(f64(w1), 0, "e4m3").T @ v
    a = h[:, unstriped(pos1)]
    gelu = f64(gain)[:, None] * a * (1.0 + np.tanh(0.7978845608 * (a + 0.044715 * a * a * a)))
    z = gelu + f64(b)[:, None]
    w4 = unpack_weight(w4_words, w4_scales, "e2m1")
    y = w4.T @ mxq(z, 0, "e4m3")
    received = h[:, unstriped(pos2)]
    out = (y - received) / (1.0 + np.abs(y))
    return out

@@ -1,0 +1,192 @@
+from contextlib import ExitStack
+
+import concourse.mybir as mybir
+
+K, H, T, S, M = 1536, 1024, 2048, 1024, 512
+FLOPS = 2 * K * H * S + 2 * H * H * M
+
+F32 = mybir.dt.float32
+BF16 = mybir.dt.bfloat16
+I32 = mybir.dt.int32
+U32 = mybir.dt.uint32
+U16 = mybir.dt.uint16
+U8 = mybir.dt.uint8
+FP8X4 = mybir.dt.float8_e4m3fn_x4
+FP4X4 = mybir.dt.float4_e2m1fn_x4
+ACT = mybir.ActivationFunctionType
+ALU = mybir.AluOpType
+
+P = 128
+PACK = 4
+KP = P * PACK
+NB = 512
+
+
+def tile_list_mill_delivery_gap_kernel(tc, tab_words, tab_scales, offs, w1, pos1, gain, b, w4_words, w4_scales, pos2, out):
+    nc = tc.nc
+    ka = K // KP
+    hb = H // KP
+    with ExitStack() as ctx:
+        keep = ctx.enter_context(tc.tile_pool(name="keep", bufs=1))
+        ring = ctx.enter_context(tc.tile_pool(name="ring", bufs=2))
+        psum = ctx.enter_context(tc.psum_pool(name="psum", bufs=1))
+
+        offs_sb = keep.tile([P, S // 16], U16, name="offs_sb")
+        pos1_sb = keep.tile([P, M // 16], U16, name="pos1_sb")
+        pos2_sb = keep.tile([P, M // 16], U16, name="pos2_sb")
+        tab_sc = keep.tile([P, T], U8, name="tab_sc", align_bytes=64)
+        w4_sc_raw = keep.tile([P, hb, H], U8, name="w4_sc_raw", align_bytes=64)
+        zero = keep.tile([P, 1], F32, name="zero")
+        zero_bias = keep.tile([P, 1], F32, name="zero_bias")
+        nc.gpsimd.memset(tab_sc[:].bitcast(I32), 0)
+        nc.gpsimd.memset(zero[:], 0.0)
+        nc.gpsimd.memset(w4_sc_raw[:].rearrange("p a n -> p (a n)").bitcast(I32), 0)
+        nc.scalar.activation(zero_bias[:], zero[:], ACT.Gelu_apprx_tanh)
+
+        nc.sync.dma_start(offs_sb[:], offs)
+        tab_sb = [keep.tile([P, T], I32, name="tab%d" % a, align_bytes=64) for a in range(ka)]
+        w_raw = {}
+        for bb in range(hb):
+            for a in range(ka):
+                w_raw[bb, a] = keep.tile([P, PACK, KP], F32, name="wraw%d%d" % (bb, a))
+
+        def load_w(bb, a):
+            nc.sync.dma_start(w_raw[bb, a][:], w1[a * KP:(a + 1) * KP, bb * KP:(bb + 1) * KP].rearrange("(p j) c -> p j c", j=PACK))
+
+        def load_tab(a, pieces):
+            words = tab_words[a].rearrange("p n i -> p (n i)").bitcast(I32)
+            for i in range(pieces):
+                cols = slice(i * T // pieces, (i + 1) * T // pieces)
+                nc.sync.dma_start(tab_sb[a][:, cols], words[:, cols])
+
+        load_tab(0, 4)
+        nc.sync.dma_start(pos1_sb[:], pos1)
+        nc.sync.dma_start(pos2_sb[:], pos2)
+        load_w(0, 0)
+        gain_sb = keep.tile([P, hb, PACK], F32, name="gain_sb")
+        nc.sync.dma_start(gain_sb[:], gain.rearrange("(c p t) -> p c t", p=P, t=PACK))
+        for q in range(4):
+            nc.sync.dma_start(tab_sc[32 * q:32 * q + 4 * ka, :].bitcast(I32), tab_scales[:, 4 * q:4 * q + 4, :].bitcast(I32))
+        load_w(0, 1)
+        load_tab(1, 1)
+        load_tab(2, 1)
+        load_w(0, 2)
+        w4_raw = keep.tile([P, hb, H // 2], I32, name="w4_raw", align_bytes=64)
+        b_sb = keep.tile([P, hb, PACK], F32, name="b_sb")
+        nc.sync.dma_start(w4_raw[:], w4_words.rearrange("a p n -> p a n").bitcast(I32))
+        load_w(1, 0)
+        for q in range(4):
+            nc.sync.dma_start(w4_sc_raw[32 * q:32 * q + 4].bitcast(I32), w4_scales[:, 4 * q:4 * q + 4, :].rearrange("a r n -> r a n").bitcast(I32))
+        load_w(1, 1)
+        load_w(1, 2)
+        nc.sync.dma_start(b_sb[:], b.rearrange("(c p t) -> p c t", p=P, t=PACK))
+
+        v_words = [keep.tile([P, S], U32, name="v%d" % a, align_bytes=64) for a in range(ka)]
+        v_sc = keep.tile([P, S], U8, name="v_sc", align_bytes=64)
+        w_codes = {}
+        w_sc = {}
+
+        def quant_w(bb, a, vector_share):
+            grouped = ring.tile([P, PACK * KP], BF16, name="grouped", align_bytes=64)
+            dst = grouped[:].rearrange("p (t m j) -> p m j t", t=PACK, j=PACK)
+            src = w_raw[bb, a][:].rearrange("p j (m t) -> p m j t", t=PACK)
+            cut = P - vector_share
+            if cut > 0:
+                nc.scalar.activation(dst[:, 0:cut], src[:, 0:cut], ACT.Copy)
+            if cut < P:
+                nc.vector.tensor_copy(dst[:, cut:P], src[:, cut:P])
+            w_codes[bb, a] = keep.tile([P, KP], U32, name="wc%d%d" % (bb, a), align_bytes=64)
+            w_sc[bb, a] = keep.tile([P, KP], U8, name="ws%d%d" % (bb, a), align_bytes=64)
+            nc.vector.quantize_mx(out=w_codes[bb, a][:].bitcast(FP8X4), scales=w_sc[bb, a][:], in_=grouped[:])
+
+        def h_pass(banks, bb, a):
+            for t in range(PACK):
+                for half in range(2):
+                    cols = slice(t * P, (t + 1) * P)
+                    ncols = slice(half * NB, (half + 1) * NB)
+                    nc.tensor.matmul_mx(out=banks[2 * t + half][:], lhsT=w_codes[bb, a][:, cols].bitcast(FP8X4), lhsT_scale=w_sc[bb, a][:, cols],
+                                        rhs=v_words[a][:, ncols].bitcast(FP8X4), rhs_scale=v_sc[4 * a:P, ncols], start=(a == 0), stop=(a == ka - 1))
+
+        def new_banks():
+            return [psum.tile([P, NB], F32, name="bank%d" % i) for i in range(8)]
+
+        h_sb = {}
+        x_sb = {}
+
+        def evac_and_pick(banks, bb):
+            x_sb[bb] = keep.tile([P, PACK, M], F32, name="x%d" % bb)
+            for t in range(PACK):
+                h_sb[bb, t] = keep.tile([P, S], F32, name="h%d%d" % (bb, t))
+                for half in range(2):
+                    nc.scalar.copy(h_sb[bb, t][:, half * NB:(half + 1) * NB], banks[2 * t + half][:])
+                nc.vector.tensor_copy(x_sb[bb][:, t, :], h_sb[bb, t][:].indirect(pos1_sb[:]))
+
+        z_codes = {}
+        z_sc = {}
+
+        def make_z(bb):
+            z_rows = keep.tile([P, PACK, M], BF16, name="z_rows", tag="z_rows", align_bytes=64)
+            for t in range(PACK):
+                nc.scalar.activation(x_sb[bb][:, t, :], x_sb[bb][:, t, :], ACT.Gelu_apprx_tanh)
+                nc.vector.tensor_scalar(z_rows[:, t, :], x_sb[bb][:, t, :], gain2[:, bb, t:t + 1], b_sb[:, bb, t:t + 1], ALU.mult, ALU.add)
+            grouped = keep.tile([P, PACK * M], BF16, name="zg%d" % bb, tag="zg%d" % bb, align_bytes=64)
+            nc.vector.tensor_copy(grouped[:].rearrange("p (c i t) -> p c t i", i=4, t=PACK), z_rows[:].rearrange("p t (c i) -> p c t i", i=4))
+            z_codes[bb] = keep.tile([P, M], U32, name="zc%d" % bb, align_bytes=64)
+            z_sc[bb] = keep.tile([P, M], U8, name="zs%d" % bb, align_bytes=64)
+            nc.vector.quantize_mx(out=z_codes[bb][:].bitcast(FP8X4), scales=z_sc[bb][:], in_=grouped[:])
+
+        banks0 = new_banks()
+        for a in range(ka):
+            pieces = 2 if a == ka - 1 else 1
+            for i in range(pieces):
+                nc.vector.tensor_copy(v_words[a][:, i * S // pieces:(i + 1) * S // pieces],
+                                      tab_sb[a][:].bitcast(U32).indirect(offs_sb[:, i * S // 16 // pieces:(i + 1) * S // 16 // pieces]))
+            if a == 0:
+                nc.vector.tensor_copy(v_sc[:], tab_sc[:].indirect(offs_sb[:]))
+            quant_w(0, a, 0)
+            h_pass(banks0, 0, a)
+
+        evac_and_pick(banks0, 0)
+        banks1 = new_banks()
+        for a in range(ka - 1):
+            quant_w(1, a, 64)
+            h_pass(banks1, 1, a)
+        gain2 = keep.tile([P, hb, PACK], F32, name="gain2")
+        nc.vector.tensor_scalar(gain2[:], gain_sb[:], 2.0, None, ALU.mult)
+        make_z(0)
+        quant_w(1, ka - 1, 0)
+        h_pass(banks1, 1, ka - 1)
+        w4_perm = keep.tile([P, hb, H], U16, name="w4_perm", align_bytes=64)
+        w4_sc = keep.tile([P, hb, H], U8, name="w4_sc", align_bytes=64)
+        nc.vector.tensor_copy(w4_perm[:].rearrange("p a (t m) -> p a m t", t=PACK),
+                              w4_raw[:].rearrange("p a n -> p (a n)").bitcast(U16).rearrange("p (a m t) -> p a m t", a=hb, t=PACK))
+        nc.vector.tensor_copy(w4_sc[:].rearrange("p a (t m) -> p a m t", t=PACK), w4_sc_raw[:].rearrange("p a (m t) -> p a m t", t=PACK))
+
+        evac_and_pick(banks1, 1)
+        make_z(1)
+
+        banks_y = new_banks()
+        for a in range(hb):
+            for i in range(8):
+                bb, t = divmod(i, PACK)
+                c0 = t * (H // PACK) + bb * P
+                nc.tensor.matmul_mx(out=banks_y[i][:], lhsT=w4_perm[:, a, c0:c0 + P].bitcast(U8).bitcast(FP4X4), lhsT_scale=w4_sc[:, a, c0:c0 + P],
+                                    rhs=z_codes[a][:].bitcast(FP8X4), rhs_scale=z_sc[a][:], start=(a == 0), stop=(a == hb - 1))
+
+        out_v = out.rearrange("(c p t) m -> c p t m", p=P, t=PACK)
+        gap_a = keep.tile([P, 2, M], F32, name="gap_a", tag="zg0", align_bytes=64)
+        gap_b = keep.tile([P, 2, M], F32, name="gap_b", tag="z_rows", align_bytes=64)
+        gap_c = keep.tile([P, 4, M], F32, name="gap_c", tag="zg1", align_bytes=64)
+        groups = [(0, 0, 2, gap_a[:]), (0, 2, 2, gap_b[:]), (1, 0, 2, gap_c[:, 0:2, :]), (1, 2, 1, gap_c[:, 2:3, :]), (1, 3, 1, gap_c[:, 3:4, :])]
+        for bb, t0, n, gap in groups:
+            inv = keep.tile([P, n, M], F32, name="inv%d%d" % (bb, t0))
+            for u in range(n):
+                nc.vector.tensor_copy(gap[:, u, :], h_sb[bb, t0 + u][:].indirect(pos2_sb[:]))
+            for u in range(n):
+                bank = banks_y[bb * PACK + t0 + u]
+                nc.scalar.activation(inv[:, u, :], bank[:], ACT.Abs, bias=zero_bias[:])
+                nc.vector.tensor_tensor(gap[:, u, :], bank[:], gap[:, u, :], ALU.subtract)
+            nc.scalar.activation(inv[:], inv[:], ACT.Abs_reciprocal_sqrt, bias=1.0)
+            nc.scalar.activation(inv[:], inv[:], ACT.Square)
+            nc.vector.tensor_tensor(gap, gap, inv[:], ALU.mult)
+            nc.sync.dma_start(out_v[bb, :, t0:t0 + n, :], gap)

@@ -39,8 +39,8 @@ def tile_list_mill_delivery_gap_kernel(tc, tab_words, tab_scales, offs, w1, pos1
         zero = keep.tile([P, 1], F32, name="zero")
         zero_bias = keep.tile([P, 1], F32, name="zero_bias")
         nc.gpsimd.memset(tab_sc[:].bitcast(I32), 0)
-        nc.gpsimd.memset(zero[:], 0.0)
-        nc.gpsimd.memset(w4_sc_raw[:].rearrange("p a n -> p (a n)").bitcast(I32), 0)
+        nc.vector.memset(w4_sc_raw[:].rearrange("p a n -> p (a n)").bitcast(I32), 0)
+        nc.vector.memset(zero[:], 0.0)
         nc.scalar.activation(zero_bias[:], zero[:], ACT.Gelu_apprx_tanh)
 
         nc.sync.dma_start(offs_sb[:], offs)
@@ -59,26 +59,25 @@ def tile_list_mill_delivery_gap_kernel(tc, tab_words, tab_scales, offs, w1, pos1
                 cols = slice(i * T // pieces, (i + 1) * T // pieces)
                 nc.sync.dma_start(tab_sb[a][:, cols], words[:, cols])
 
+        for q in range(4):
+            nc.gpsimd.dma_start(tab_sc[32 * q:32 * q + 4 * ka, :].bitcast(I32), tab_scales[:, 4 * q:4 * q + 4, :].bitcast(I32))
         load_tab(0, 4)
         nc.sync.dma_start(pos1_sb[:], pos1)
         nc.sync.dma_start(pos2_sb[:], pos2)
         load_w(0, 0)
         gain_sb = keep.tile([P, hb, PACK], F32, name="gain_sb")
+        b_sb = keep.tile([P, hb, PACK], F32, name="b_sb")
         nc.sync.dma_start(gain_sb[:], gain.rearrange("(c p t) -> p c t", p=P, t=PACK))
         for q in range(4):
-            nc.sync.dma_start(tab_sc[32 * q:32 * q + 4 * ka, :].bitcast(I32), tab_scales[:, 4 * q:4 * q + 4, :].bitcast(I32))
+            nc.sync.dma_start(w4_sc_raw[32 * q:32 * q + 4].bitcast(I32), w4_scales[:, 4 * q:4 * q + 4, :].rearrange("a r n -> r a n").bitcast(I32))
+        w4_raw = keep.tile([P, hb, H // 2], I32, name="w4_raw", align_bytes=64)
+        nc.sync.dma_start(w4_raw[:], w4_words.rearrange("a p n -> p a n").bitcast(I32))
         load_w(0, 1)
         load_tab(1, 1)
         load_tab(2, 1)
         load_w(0, 2)
-        w4_raw = keep.tile([P, hb, H // 2], I32, name="w4_raw", align_bytes=64)
-        b_sb = keep.tile([P, hb, PACK], F32, name="b_sb")
-        nc.sync.dma_start(w4_raw[:], w4_words.rearrange("a p n -> p a n").bitcast(I32))
-        load_w(1, 0)
-        for q in range(4):
-            nc.sync.dma_start(w4_sc_raw[32 * q:32 * q + 4].bitcast(I32), w4_scales[:, 4 * q:4 * q + 4, :].rearrange("a r n -> r a n").bitcast(I32))
-        load_w(1, 1)
-        load_w(1, 2)
+        for a in range(ka):
+            load_w(1, a)
         nc.sync.dma_start(b_sb[:], b.rearrange("(c p t) -> p c t", p=P, t=PACK))
 
         v_words = [keep.tile([P, S], U32, name="v%d" % a, align_bytes=64) for a in range(ka)]
@@ -137,56 +136,51 @@ def tile_list_mill_delivery_gap_kernel(tc, tab_words, tab_scales, offs, w1, pos1
 
         banks0 = new_banks()
         for a in range(ka):
-            pieces = 2 if a == ka - 1 else 1
-            for i in range(pieces):
-                nc.vector.tensor_copy(v_words[a][:, i * S // pieces:(i + 1) * S // pieces],
-                                      tab_sb[a][:].bitcast(U32).indirect(offs_sb[:, i * S // 16 // pieces:(i + 1) * S // 16 // pieces]))
+            nc.vector.tensor_copy(v_words[a][:], tab_sb[a][:].bitcast(U32).indirect(offs_sb[:]))
             if a == 0:
                 nc.vector.tensor_copy(v_sc[:], tab_sc[:].indirect(offs_sb[:]))
-            quant_w(0, a, 0)
+            quant_w(0, a, 32 if a == ka - 1 else 0)
             h_pass(banks0, 0, a)
 
         evac_and_pick(banks0, 0)
         banks1 = new_banks()
-        for a in range(ka - 1):
-            quant_w(1, a, 64)
+        for a in range(ka):
+            quant_w(1, a, 0 if a == ka - 1 else P)
             h_pass(banks1, 1, a)
         gain2 = keep.tile([P, hb, PACK], F32, name="gain2")
         nc.vector.tensor_scalar(gain2[:], gain_sb[:], 2.0, None, ALU.mult)
         make_z(0)
-        quant_w(1, ka - 1, 0)
-        h_pass(banks1, 1, ka - 1)
-        w4_perm = keep.tile([P, hb, H], U16, name="w4_perm", align_bytes=64)
-        w4_sc = keep.tile([P, hb, H], U8, name="w4_sc", align_bytes=64)
-        nc.vector.tensor_copy(w4_perm[:].rearrange("p a (t m) -> p a m t", t=PACK),
-                              w4_raw[:].rearrange("p a n -> p (a n)").bitcast(U16).rearrange("p (a m t) -> p a m t", a=hb, t=PACK))
-        nc.vector.tensor_copy(w4_sc[:].rearrange("p a (t m) -> p a m t", t=PACK), w4_sc_raw[:].rearrange("p a (m t) -> p a m t", t=PACK))
+        w4_perm = keep.tile([P, PACK, hb, H // PACK], U16, name="w4_perm", align_bytes=64)
+        w4_sc = keep.tile([P, PACK, hb, H // PACK], U8, name="w4_sc", align_bytes=64)
+        nc.vector.tensor_copy(w4_perm[:].rearrange("p t a (g i) -> p (a g) t i", i=8),
+                              w4_raw[:].rearrange("p a n -> p (a n)").bitcast(U16).rearrange("p (g i t) -> p g t i", i=8, t=PACK))
+        nc.vector.tensor_copy(w4_sc[:].rearrange("p t a (g i) -> p (a g) t i", i=16),
+                              w4_sc_raw[:].rearrange("p a (g i t) -> p (a g) t i", i=16, t=PACK))
 
         evac_and_pick(banks1, 1)
         make_z(1)
+        table_warm = keep.tile([P, 1], F32, name="table_warm")
+        nc.scalar.activation(table_warm[:], x_sb[1][:, PACK - 1, 0:1], ACT.Abs_reciprocal_sqrt, bias=1.0, scale=0.0)
 
         banks_y = new_banks()
         for a in range(hb):
             for i in range(8):
                 bb, t = divmod(i, PACK)
-                c0 = t * (H // PACK) + bb * P
-                nc.tensor.matmul_mx(out=banks_y[i][:], lhsT=w4_perm[:, a, c0:c0 + P].bitcast(U8).bitcast(FP4X4), lhsT_scale=w4_sc[:, a, c0:c0 + P],
+                c0 = bb * P
+                nc.tensor.matmul_mx(out=banks_y[i][:], lhsT=w4_perm[:, t, a, c0:c0 + P].bitcast(U8).bitcast(FP4X4), lhsT_scale=w4_sc[:, t, a, c0:c0 + P],
                                     rhs=z_codes[a][:].bitcast(FP8X4), rhs_scale=z_sc[a][:], start=(a == 0), stop=(a == hb - 1))
 
         out_v = out.rearrange("(c p t) m -> c p t m", p=P, t=PACK)
-        gap_a = keep.tile([P, 2, M], F32, name="gap_a", tag="zg0", align_bytes=64)
-        gap_b = keep.tile([P, 2, M], F32, name="gap_b", tag="z_rows", align_bytes=64)
-        gap_c = keep.tile([P, 4, M], F32, name="gap_c", tag="zg1", align_bytes=64)
-        groups = [(0, 0, 2, gap_a[:]), (0, 2, 2, gap_b[:]), (1, 0, 2, gap_c[:, 0:2, :]), (1, 2, 1, gap_c[:, 2:3, :]), (1, 3, 1, gap_c[:, 3:4, :])]
-        for bb, t0, n, gap in groups:
-            inv = keep.tile([P, n, M], F32, name="inv%d%d" % (bb, t0))
-            for u in range(n):
-                nc.vector.tensor_copy(gap[:, u, :], h_sb[bb, t0 + u][:].indirect(pos2_sb[:]))
-            for u in range(n):
-                bank = banks_y[bb * PACK + t0 + u]
-                nc.scalar.activation(inv[:, u, :], bank[:], ACT.Abs, bias=zero_bias[:])
-                nc.vector.tensor_tensor(gap[:, u, :], bank[:], gap[:, u, :], ALU.subtract)
+        for i in range(8):
+            bb, t = divmod(i, PACK)
+            received = keep.tile([P, M], F32, name="received", tag="zg1" if i % 2 else "z_rows", align_bytes=64)
+            gap = keep.tile([P, M], F32, name="gap%d" % i)
+            inv = keep.tile([P, M], F32, name="inv%d" % i)
+            nc.vector.tensor_copy(received[:], h_sb[bb, t][:].indirect(pos2_sb[:]))
+            nc.scalar.activation(inv[:], banks_y[i][:], ACT.Abs, bias=zero_bias[:])
+            nc.vector.tensor_tensor(gap[:], banks_y[i][:], received[:], ALU.subtract)
             nc.scalar.activation(inv[:], inv[:], ACT.Abs_reciprocal_sqrt, bias=1.0)
             nc.scalar.activation(inv[:], inv[:], ACT.Square)
-            nc.vector.tensor_tensor(gap, gap, inv[:], ALU.mult)
-            nc.sync.dma_start(out_v[bb, :, t0:t0 + n, :], gap)
+            engine = nc.gpsimd if i < 6 else nc.vector
+            engine.tensor_tensor(gap[:], gap[:], inv[:], ALU.mult)
+            nc.sync.dma_start(out_v[bb, :, t, :], gap[:])

@@ -117,7 +117,10 @@ def tile_list_mill_delivery_gap_kernel(tc, tab_words, tab_scales, offs, w1, pos1
             for t in range(PACK):
                 h_sb[bb, t] = keep.tile([P, S], F32, name="h%d%d" % (bb, t))
                 for half in range(2):
-                    nc.scalar.copy(h_sb[bb, t][:, half * NB:(half + 1) * NB], banks[2 * t + half][:])
+                    if (bb, t, half) == (1, 0, 1):
+                        nc.vector.tensor_copy(h_sb[bb, t][:, half * NB:(half + 1) * NB], banks[2 * t + half][:])
+                    else:
+                        nc.scalar.copy(h_sb[bb, t][:, half * NB:(half + 1) * NB], banks[2 * t + half][:])
                 nc.vector.tensor_copy(x_sb[bb][:, t, :], h_sb[bb, t][:].indirect(pos1_sb[:]))
 
         z_codes = {}
@@ -127,9 +130,12 @@ def tile_list_mill_delivery_gap_kernel(tc, tab_words, tab_scales, offs, w1, pos1
             z_rows = keep.tile([P, PACK, M], BF16, name="z_rows", tag="z_rows", align_bytes=64)
             for t in range(PACK):
                 nc.scalar.activation(x_sb[bb][:, t, :], x_sb[bb][:, t, :], ACT.Gelu_apprx_tanh)
-                nc.vector.tensor_scalar(z_rows[:, t, :], x_sb[bb][:, t, :], gain2[:, bb, t:t + 1], b_sb[:, bb, t:t + 1], ALU.mult, ALU.add)
+                nc.gpsimd.tensor_scalar(z_rows[:, t, :], x_sb[bb][:, t, :], gain2[:, bb, t:t + 1], b_sb[:, bb, t:t + 1], ALU.mult, ALU.add)
             grouped = keep.tile([P, PACK * M], BF16, name="zg%d" % bb, tag="zg%d" % bb, align_bytes=64)
-            nc.vector.tensor_copy(grouped[:].rearrange("p (c i t) -> p c t i", i=4, t=PACK), z_rows[:].rearrange("p t (c i) -> p c t i", i=4))
+            if bb == 0:
+                nc.gpsimd.tensor_scalar(grouped[:].rearrange("p (m t) -> p m t", t=PACK), z_rows[:].rearrange("p t m -> p m t"), 1.0, 0.0, ALU.mult, ALU.add)
+            else:
+                nc.vector.tensor_copy(grouped[:].rearrange("p (c i t) -> p c t i", i=4, t=PACK), z_rows[:].rearrange("p t (c i) -> p c t i", i=4))
             z_codes[bb] = keep.tile([P, M], U32, name="zc%d" % bb, align_bytes=64)
             z_sc[bb] = keep.tile([P, M], U8, name="zs%d" % bb, align_bytes=64)
             nc.vector.quantize_mx(out=z_codes[bb][:].bitcast(FP8X4), scales=z_sc[bb][:], in_=grouped[:])
@@ -145,10 +151,10 @@ def tile_list_mill_delivery_gap_kernel(tc, tab_words, tab_scales, offs, w1, pos1
         evac_and_pick(banks0, 0)
         banks1 = new_banks()
         for a in range(ka):
-            quant_w(1, a, 0 if a == ka - 1 else P)
+            quant_w(1, a, (64, P, 0)[a])
             h_pass(banks1, 1, a)
         gain2 = keep.tile([P, hb, PACK], F32, name="gain2")
-        nc.vector.tensor_scalar(gain2[:], gain_sb[:], 2.0, None, ALU.mult)
+        nc.gpsimd.tensor_scalar(gain2[:], gain_sb[:], 2.0, 0.0, ALU.mult, ALU.add)
         make_z(0)
         w4_perm = keep.tile([P, PACK, hb, H // PACK], U16, name="w4_perm", align_bytes=64)
         w4_sc = keep.tile([P, PACK, hb, H // PACK], U8, name="w4_sc", align_bytes=64)
@@ -173,14 +179,17 @@ def tile_list_mill_delivery_gap_kernel(tc, tab_words, tab_scales, offs, w1, pos1
         out_v = out.rearrange("(c p t) m -> c p t m", p=P, t=PACK)
         for i in range(8):
             bb, t = divmod(i, PACK)
-            received = keep.tile([P, M], F32, name="received", tag="zg1" if i % 2 else "z_rows", align_bytes=64)
+            received = keep.tile([P, M], F32, name="received", tag=("zg0", "z_rows", "zg1")[i % 3], align_bytes=64)
             gap = keep.tile([P, M], F32, name="gap%d" % i)
             inv = keep.tile([P, M], F32, name="inv%d" % i)
             nc.vector.tensor_copy(received[:], h_sb[bb, t][:].indirect(pos2_sb[:]))
             nc.scalar.activation(inv[:], banks_y[i][:], ACT.Abs, bias=zero_bias[:])
             nc.vector.tensor_tensor(gap[:], banks_y[i][:], received[:], ALU.subtract)
             nc.scalar.activation(inv[:], inv[:], ACT.Abs_reciprocal_sqrt, bias=1.0)
-            nc.scalar.activation(inv[:], inv[:], ACT.Square)
+            if i == 1:
+                nc.gpsimd.tensor_tensor(gap[:], gap[:], inv[:], ALU.mult)
+            else:
+                nc.scalar.activation(inv[:], inv[:], ACT.Square)
             engine = nc.gpsimd if i < 6 else nc.vector
             engine.tensor_tensor(gap[:], gap[:], inv[:], ALU.mult)
             nc.sync.dma_start(out_v[bb, :, t, :], gap[:])

@@ -113,15 +113,12 @@ def tile_list_mill_delivery_gap_kernel(tc, tab_words, tab_scales, offs, w1, pos1
         x_sb = {}
 
         def evac_and_pick(banks, bb):
-            x_sb[bb] = keep.tile([P, PACK, M], F32, name="x%d" % bb)
             for t in range(PACK):
                 h_sb[bb, t] = keep.tile([P, S], F32, name="h%d%d" % (bb, t))
                 for half in range(2):
-                    if (bb, t, half) == (1, 0, 1):
-                        nc.vector.tensor_copy(h_sb[bb, t][:, half * NB:(half + 1) * NB], banks[2 * t + half][:])
-                    else:
-                        nc.scalar.copy(h_sb[bb, t][:, half * NB:(half + 1) * NB], banks[2 * t + half][:])
-                nc.vector.tensor_copy(x_sb[bb][:, t, :], h_sb[bb, t][:].indirect(pos1_sb[:]))
+                    nc.scalar.copy(h_sb[bb, t][:, half * NB:(half + 1) * NB], banks[2 * t + half][:])
+                x_sb[bb, t] = keep.tile([P, M], F32, name="x%d%d" % (bb, t), tag="x%d%d" % (bb, t), align_bytes=64)
+                nc.vector.tensor_copy(x_sb[bb, t][:], h_sb[bb, t][:].indirect(pos1_sb[:]))
 
         z_codes = {}
         z_sc = {}
@@ -129,13 +126,10 @@ def tile_list_mill_delivery_gap_kernel(tc, tab_words, tab_scales, offs, w1, pos1
         def make_z(bb):
             z_rows = keep.tile([P, PACK, M], BF16, name="z_rows", tag="z_rows", align_bytes=64)
             for t in range(PACK):
-                nc.scalar.activation(x_sb[bb][:, t, :], x_sb[bb][:, t, :], ACT.Gelu_apprx_tanh)
-                nc.gpsimd.tensor_scalar(z_rows[:, t, :], x_sb[bb][:, t, :], gain2[:, bb, t:t + 1], b_sb[:, bb, t:t + 1], ALU.mult, ALU.add)
+                nc.scalar.activation(x_sb[bb, t][:], x_sb[bb, t][:], ACT.Gelu_apprx_tanh)
+                (nc.gpsimd if bb else nc.vector).tensor_scalar(z_rows[:, t, :], x_sb[bb, t][:], gain2[:, bb, t:t + 1], b_sb[:, bb, t:t + 1], ALU.mult, ALU.add)
             grouped = keep.tile([P, PACK * M], BF16, name="zg%d" % bb, tag="zg%d" % bb, align_bytes=64)
-            if bb == 0:
-                nc.gpsimd.tensor_scalar(grouped[:].rearrange("p (m t) -> p m t", t=PACK), z_rows[:].rearrange("p t m -> p m t"), 1.0, 0.0, ALU.mult, ALU.add)
-            else:
-                nc.vector.tensor_copy(grouped[:].rearrange("p (c i t) -> p c t i", i=4, t=PACK), z_rows[:].rearrange("p t (c i) -> p c t i", i=4))
+            nc.vector.tensor_copy(grouped[:].rearrange("p (c i t) -> p c t i", i=4, t=PACK), z_rows[:].rearrange("p t (c i) -> p c t i", i=4))
             z_codes[bb] = keep.tile([P, M], U32, name="zc%d" % bb, align_bytes=64)
             z_sc[bb] = keep.tile([P, M], U8, name="zs%d" % bb, align_bytes=64)
             nc.vector.quantize_mx(out=z_codes[bb][:].bitcast(FP8X4), scales=z_sc[bb][:], in_=grouped[:])
@@ -148,6 +142,13 @@ def tile_list_mill_delivery_gap_kernel(tc, tab_words, tab_scales, offs, w1, pos1
             quant_w(0, a, 32 if a == ka - 1 else 0)
             h_pass(banks0, 0, a)
 
+        w4_perm = keep.tile([P, PACK, hb, H // PACK], U16, name="w4_perm", align_bytes=64)
+        w4_sc = keep.tile([P, PACK, hb, H // PACK], U8, name="w4_sc", align_bytes=64)
+        nc.vector.tensor_copy(w4_perm[:].rearrange("p t a (g i) -> p (a g) t i", i=8),
+                              w4_raw[:].rearrange("p a n -> p (a n)").bitcast(U16).rearrange("p (g i t) -> p g t i", i=8, t=PACK))
+        nc.vector.tensor_copy(w4_sc[:].rearrange("p t a (g i) -> p (a g) t i", i=16),
+                              w4_sc_raw[:].rearrange("p a (g i t) -> p (a g) t i", i=16, t=PACK))
+
         evac_and_pick(banks0, 0)
         banks1 = new_banks()
         for a in range(ka):
@@ -156,17 +157,10 @@ def tile_list_mill_delivery_gap_kernel(tc, tab_words, tab_scales, offs, w1, pos1
         gain2 = keep.tile([P, hb, PACK], F32, name="gain2")
         nc.gpsimd.tensor_scalar(gain2[:], gain_sb[:], 2.0, 0.0, ALU.mult, ALU.add)
         make_z(0)
-        w4_perm = keep.tile([P, PACK, hb, H // PACK], U16, name="w4_perm", align_bytes=64)
-        w4_sc = keep.tile([P, PACK, hb, H // PACK], U8, name="w4_sc", align_bytes=64)
-        nc.vector.tensor_copy(w4_perm[:].rearrange("p t a (g i) -> p (a g) t i", i=8),
-                              w4_raw[:].rearrange("p a n -> p (a n)").bitcast(U16).rearrange("p (g i t) -> p g t i", i=8, t=PACK))
-        nc.vector.tensor_copy(w4_sc[:].rearrange("p t a (g i) -> p (a g) t i", i=16),
-                              w4_sc_raw[:].rearrange("p a (g i t) -> p (a g) t i", i=16, t=PACK))
-
         evac_and_pick(banks1, 1)
         make_z(1)
         table_warm = keep.tile([P, 1], F32, name="table_warm")
-        nc.scalar.activation(table_warm[:], x_sb[1][:, PACK - 1, 0:1], ACT.Abs_reciprocal_sqrt, bias=1.0, scale=0.0)
+        nc.scalar.activation(table_warm[:], x_sb[1, PACK - 1][:, 0:1], ACT.Abs_reciprocal_sqrt, bias=1.0, scale=0.0)
 
         banks_y = new_banks()
         for a in range(hb):
@@ -179,7 +173,7 @@ def tile_list_mill_delivery_gap_kernel(tc, tab_words, tab_scales, offs, w1, pos1
         out_v = out.rearrange("(c p t) m -> c p t m", p=P, t=PACK)
         for i in range(8):
             bb, t = divmod(i, PACK)
-            received = keep.tile([P, M], F32, name="received", tag=("zg0", "z_rows", "zg1")[i % 3], align_bytes=64)
+            received = keep.tile([P, M], F32, name="received", tag=("x12", "z_rows", "zg1")[i % 3], align_bytes=64)
             gap = keep.tile([P, M], F32, name="gap%d" % i)
             inv = keep.tile([P, M], F32, name="inv%d" % i)
             nc.vector.tensor_copy(received[:], h_sb[bb, t][:].indirect(pos2_sb[:]))

@@ -28,78 +28,95 @@ def tile_list_mill_delivery_gap_kernel(tc, tab_words, tab_scales, offs, w1, pos1
     hb = H // KP
     with ExitStack() as ctx:
         keep = ctx.enter_context(tc.tile_pool(name="keep", bufs=1))
-        ring = ctx.enter_context(tc.tile_pool(name="ring", bufs=2))
         psum = ctx.enter_context(tc.psum_pool(name="psum", bufs=1))
 
         offs_sb = keep.tile([P, S // 16], U16, name="offs_sb")
         pos1_sb = keep.tile([P, M // 16], U16, name="pos1_sb")
         pos2_sb = keep.tile([P, M // 16], U16, name="pos2_sb")
         tab_sc = keep.tile([P, T], U8, name="tab_sc", align_bytes=64)
-        w4_sc_raw = keep.tile([P, hb, H], U8, name="w4_sc_raw", align_bytes=64)
+        w4_sc_raw = keep.tile([P, H], U8, name="w4_sc_raw", align_bytes=64)
+        w4_sc = {1: keep.tile([P, PACK, H // PACK], U8, name="w4_sc1", align_bytes=64)}
         zero = keep.tile([P, 1], F32, name="zero")
         zero_bias = keep.tile([P, 1], F32, name="zero_bias")
-        nc.gpsimd.memset(tab_sc[:].bitcast(I32), 0)
-        nc.vector.memset(w4_sc_raw[:].rearrange("p a n -> p (a n)").bitcast(I32), 0)
+        nc.vector.memset(tab_sc[:].bitcast(I32), 0)
         nc.vector.memset(zero[:], 0.0)
-        nc.scalar.activation(zero_bias[:], zero[:], ACT.Gelu_apprx_tanh)
+        nc.vector.memset(w4_sc_raw[:].bitcast(I32), 0)
+        nc.vector.memset(w4_sc[1][:].rearrange("p t n -> p (t n)").bitcast(I32), 0)
 
-        nc.sync.dma_start(offs_sb[:], offs)
         tab_sb = [keep.tile([P, T], I32, name="tab%d" % a, align_bytes=64) for a in range(ka)]
         w_raw = {}
         for bb in range(hb):
             for a in range(ka):
-                w_raw[bb, a] = keep.tile([P, PACK, KP], F32, name="wraw%d%d" % (bb, a))
+                w_raw[bb, a] = keep.tile([P, PACK, KP], F32, name="wraw%d%d" % (bb, a), tag="wraw%d%d" % (bb, a), align_bytes=64)
 
         def load_w(bb, a):
             nc.sync.dma_start(w_raw[bb, a][:], w1[a * KP:(a + 1) * KP, bb * KP:(bb + 1) * KP].rearrange("(p j) c -> p j c", j=PACK))
 
-        def load_tab(a, pieces):
-            words = tab_words[a].rearrange("p n i -> p (n i)").bitcast(I32)
-            for i in range(pieces):
-                cols = slice(i * T // pieces, (i + 1) * T // pieces)
-                nc.sync.dma_start(tab_sb[a][:, cols], words[:, cols])
+        def load_tab(a):
+            nc.sync.dma_start(tab_sb[a][:], tab_words[a].rearrange("p n i -> p (n i)").bitcast(I32))
 
-        for q in range(4):
-            nc.gpsimd.dma_start(tab_sc[32 * q:32 * q + 4 * ka, :].bitcast(I32), tab_scales[:, 4 * q:4 * q + 4, :].bitcast(I32))
-        load_tab(0, 4)
-        nc.sync.dma_start(pos1_sb[:], pos1)
-        nc.sync.dma_start(pos2_sb[:], pos2)
-        load_w(0, 0)
+        def load_w4_scales(q):
+            nc.sync.dma_start(w4_sc_raw[32 * q:32 * q + 4 * hb, :].bitcast(I32), w4_scales[:, 4 * q:4 * q + 4, :].bitcast(I32))
+
         gain_sb = keep.tile([P, hb, PACK], F32, name="gain_sb")
         b_sb = keep.tile([P, hb, PACK], F32, name="b_sb")
-        nc.sync.dma_start(gain_sb[:], gain.rearrange("(c p t) -> p c t", p=P, t=PACK))
-        for q in range(4):
-            nc.sync.dma_start(w4_sc_raw[32 * q:32 * q + 4].bitcast(I32), w4_scales[:, 4 * q:4 * q + 4, :].rearrange("a r n -> r a n").bitcast(I32))
-        w4_raw = keep.tile([P, hb, H // 2], I32, name="w4_raw", align_bytes=64)
-        nc.sync.dma_start(w4_raw[:], w4_words.rearrange("a p n -> p a n").bitcast(I32))
+        w4_raw = [keep.tile([P, H // 2], I32, name="w4_raw%d" % a, tag=("w4_raw0", "z_rows0")[a], align_bytes=64) for a in range(hb)]
+
+        nc.sync.dma_start(offs_sb[:], offs)
+        staged = keep.tile([P, T // 4], I32, name="staged", align_bytes=64)
+
+        def load_scale_rows(queue, q):
+            rows = slice(32 * q, 32 * q + 4 * ka)
+            queue.dma_start(staged[rows, :], tab_scales[:, 4 * q:4 * q + 4, :].bitcast(I32))
+            nc.vector.tensor_copy(tab_sc[rows, :].bitcast(I32), staged[rows, :])
+
+        load_scale_rows(nc.scalar, 0)
+        load_scale_rows(nc.scalar, 1)
+        load_tab(0)
+        load_scale_rows(nc.sync, 2)
+        load_scale_rows(nc.sync, 3)
+        nc.scalar.activation(zero_bias[:], zero[:], ACT.Gelu_apprx_tanh)
+        load_w(0, 0)
+        load_tab(1)
         load_w(0, 1)
-        load_tab(1, 1)
-        load_tab(2, 1)
+        for q in range(4):
+            load_w4_scales(q)
+        load_tab(2)
+        nc.sync.dma_start(pos1_sb[:], pos1)
         load_w(0, 2)
+        nc.sync.dma_start(pos2_sb[:], pos2)
+        nc.sync.dma_start(gain_sb[:], gain.rearrange("(c p t) -> p c t", p=P, t=PACK))
+        nc.sync.dma_start(b_sb[:], b.rearrange("(c p t) -> p c t", p=P, t=PACK))
         for a in range(ka):
             load_w(1, a)
-        nc.sync.dma_start(b_sb[:], b.rearrange("(c p t) -> p c t", p=P, t=PACK))
+        for a in range(hb):
+            nc.sync.dma_start(w4_raw[a][:], w4_words[a].bitcast(I32))
 
-        v_words = [keep.tile([P, S], U32, name="v%d" % a, align_bytes=64) for a in range(ka)]
+        v_words = {}
         v_sc = keep.tile([P, S], U8, name="v_sc", align_bytes=64)
         w_codes = {}
         w_sc = {}
 
-        def quant_w(bb, a, vector_share):
-            grouped = ring.tile([P, PACK * KP], BF16, name="grouped", align_bytes=64)
+        def quant_w(bb, a, shares):
+            grouped = keep.tile([P, PACK * KP], BF16, name="grouped%d%d" % (bb, a), tag="grouped0%d" % a if bb == 0 and a < 2 else "grouped%d" % a, align_bytes=64)
             dst = grouped[:].rearrange("p (t m j) -> p m j t", t=PACK, j=PACK)
             src = w_raw[bb, a][:].rearrange("p j (m t) -> p m j t", t=PACK)
-            cut = P - vector_share
-            if cut > 0:
-                nc.scalar.activation(dst[:, 0:cut], src[:, 0:cut], ACT.Copy)
-            if cut < P:
-                nc.vector.tensor_copy(dst[:, cut:P], src[:, cut:P])
+            m0 = 0
+            for engine, width in shares:
+                cols = slice(m0, m0 + width)
+                if engine == "scalar":
+                    nc.scalar.activation(dst[:, cols], src[:, cols], ACT.Copy)
+                elif engine == "vector":
+                    nc.vector.tensor_copy(dst[:, cols], src[:, cols])
+                else:
+                    nc.gpsimd.tensor_scalar(dst[:, cols].rearrange("p m j t -> p t m j"), src[:, cols].rearrange("p m j t -> p t m j"), 1.0, 0.0, ALU.mult, ALU.add)
+                m0 = m0 + width
             w_codes[bb, a] = keep.tile([P, KP], U32, name="wc%d%d" % (bb, a), align_bytes=64)
             w_sc[bb, a] = keep.tile([P, KP], U8, name="ws%d%d" % (bb, a), align_bytes=64)
             nc.vector.quantize_mx(out=w_codes[bb, a][:].bitcast(FP8X4), scales=w_sc[bb, a][:], in_=grouped[:])
 
-        def h_pass(banks, bb, a):
-            for t in range(PACK):
+        def h_pass(banks, bb, a, tiles):
+            for t in tiles:
                 for half in range(2):
                     cols = slice(t * P, (t + 1) * P)
                     ncols = slice(half * NB, (half + 1) * NB)
@@ -112,73 +129,101 @@ def tile_list_mill_delivery_gap_kernel(tc, tab_words, tab_scales, offs, w1, pos1
         h_sb = {}
         x_sb = {}
 
+        def pick(bb, t, tag):
+            x_sb[bb, t] = keep.tile([P, M], F32, name="x%d%d" % (bb, t), tag=tag, align_bytes=64)
+            nc.vector.tensor_copy(x_sb[bb, t][:], h_sb[bb, t][:].indirect(pos1_sb[:]))
+
         def evac_and_pick(banks, bb):
             for t in range(PACK):
                 h_sb[bb, t] = keep.tile([P, S], F32, name="h%d%d" % (bb, t))
                 for half in range(2):
                     nc.scalar.copy(h_sb[bb, t][:, half * NB:(half + 1) * NB], banks[2 * t + half][:])
-                x_sb[bb, t] = keep.tile([P, M], F32, name="x%d%d" % (bb, t), tag="x%d%d" % (bb, t), align_bytes=64)
-                nc.vector.tensor_copy(x_sb[bb, t][:], h_sb[bb, t][:].indirect(pos1_sb[:]))
+                if bb > 0 or t < PACK - 1:
+                    pick(bb, t, "x%d%d" % (bb, t))
 
         z_codes = {}
         z_sc = {}
+        z_rows = {}
+
+        def make_rows(bb, tiles):
+            if bb not in z_rows:
+                z_rows[bb] = keep.tile([P, PACK, M], BF16, name="z_rows%d" % bb, tag="z_rows%d" % bb, align_bytes=64)
+            for t in tiles:
+                nc.scalar.activation(x_sb[bb, t][:], x_sb[bb, t][:], ACT.Gelu_apprx_tanh)
+                last = bb == hb - 1
+                (nc.vector if last else nc.gpsimd).tensor_scalar(z_rows[bb][:, t, :], x_sb[bb, t][:], gain2[:, bb, t:t + 1], b_sb[:, bb, t:t + 1], ALU.mult, ALU.add)
 
         def make_z(bb):
-            z_rows = keep.tile([P, PACK, M], BF16, name="z_rows", tag="z_rows", align_bytes=64)
-            for t in range(PACK):
-                nc.scalar.activation(x_sb[bb, t][:], x_sb[bb, t][:], ACT.Gelu_apprx_tanh)
-                (nc.gpsimd if bb else nc.vector).tensor_scalar(z_rows[:, t, :], x_sb[bb, t][:], gain2[:, bb, t:t + 1], b_sb[:, bb, t:t + 1], ALU.mult, ALU.add)
             grouped = keep.tile([P, PACK * M], BF16, name="zg%d" % bb, tag="zg%d" % bb, align_bytes=64)
-            nc.vector.tensor_copy(grouped[:].rearrange("p (c i t) -> p c t i", i=4, t=PACK), z_rows[:].rearrange("p t (c i) -> p c t i", i=4))
-            z_codes[bb] = keep.tile([P, M], U32, name="zc%d" % bb, align_bytes=64)
+            dst = grouped[:].rearrange("p (c i t) -> p c t i", i=4, t=PACK)
+            src = z_rows[bb][:].rearrange("p t (c i) -> p c t i", i=4)
+            if bb == 0:
+                for c0 in range(0, P, 32):
+                    nc.gpsimd.tensor_scalar(dst[:, c0:c0 + 32].rearrange("p c t i -> p c i t"), src[:, c0:c0 + 32].rearrange("p c t i -> p c i t"), 1.0, 0.0, ALU.mult, ALU.add)
+            else:
+                nc.vector.tensor_copy(dst, src)
+            z_codes[bb] = keep.tile([P, M], U32, name="zc%d" % bb, tag="zc%d" % bb, align_bytes=64)
             z_sc[bb] = keep.tile([P, M], U8, name="zs%d" % bb, align_bytes=64)
             nc.vector.quantize_mx(out=z_codes[bb][:].bitcast(FP8X4), scales=z_sc[bb][:], in_=grouped[:])
 
-        banks0 = new_banks()
-        for a in range(ka):
+        def gather_words(a):
+            v_words[a] = keep.tile([P, S], U32, name="v%d" % a, tag="grouped00" if a == 1 else "v%d" % a, align_bytes=64)
             nc.vector.tensor_copy(v_words[a][:], tab_sb[a][:].bitcast(U32).indirect(offs_sb[:]))
+
+        banks0 = new_banks()
+        shares0 = ([("scalar", 128)], [("scalar", 72), ("gpsimd", 28), ("gpsimd", 28)], [("scalar", 40), ("vector", 88)])
+        for a in range(ka):
+            gather_words(a)
             if a == 0:
                 nc.vector.tensor_copy(v_sc[:], tab_sc[:].indirect(offs_sb[:]))
-            quant_w(0, a, 32 if a == ka - 1 else 0)
-            h_pass(banks0, 0, a)
+            quant_w(0, a, shares0[a])
+            h_pass(banks0, 0, a, range(PACK))
 
-        w4_perm = keep.tile([P, PACK, hb, H // PACK], U16, name="w4_perm", align_bytes=64)
-        w4_sc = keep.tile([P, PACK, hb, H // PACK], U8, name="w4_sc", align_bytes=64)
-        nc.vector.tensor_copy(w4_perm[:].rearrange("p t a (g i) -> p (a g) t i", i=8),
-                              w4_raw[:].rearrange("p a n -> p (a n)").bitcast(U16).rearrange("p (g i t) -> p g t i", i=8, t=PACK))
-        nc.vector.tensor_copy(w4_sc[:].rearrange("p t a (g i) -> p (a g) t i", i=16),
-                              w4_sc_raw[:].rearrange("p a (g i t) -> p (a g) t i", i=16, t=PACK))
-
+        w4_sc[0] = keep.tile([P, PACK, H // PACK], U8, name="w4_sc0", tag="grouped01", align_bytes=64)
+        nc.gpsimd.tensor_copy(w4_sc[0][:].rearrange("p t (g i) -> p g t i", i=16), w4_sc_raw[:].rearrange("p (g i t) -> p g t i", i=16, t=PACK))
+        for q in range(4):
+            nc.sync.dma_start(w4_sc[1][32 * q:32 * q + 4].rearrange("p t n -> p (t n)").bitcast(I32), w4_sc[0][32 * q + 4:32 * q + 8].rearrange("p t n -> p (t n)").bitcast(I32))
         evac_and_pick(banks0, 0)
-        banks1 = new_banks()
-        for a in range(ka):
-            quant_w(1, a, (64, P, 0)[a])
-            h_pass(banks1, 1, a)
         gain2 = keep.tile([P, hb, PACK], F32, name="gain2")
         nc.gpsimd.tensor_scalar(gain2[:], gain_sb[:], 2.0, 0.0, ALU.mult, ALU.add)
+        banks1 = new_banks()
+        shares1 = ([("scalar", 32), ("vector", 96)], [("gpsimd", 32)] * 4, [("scalar", 80), ("gpsimd", 24), ("gpsimd", 24)])
+        for a in range(ka):
+            quant_w(1, a, shares1[a])
+            if a == 1:
+                pick(0, PACK - 1, "grouped1")
+        for a in range(ka):
+            h_pass(banks1, 1, a, range(PACK))
+        w4_perm = keep.tile([P, hb, PACK, H // PACK], U16, name="w4_perm", tag="wraw12", align_bytes=64)
+        for a in range(hb):
+            nc.vector.tensor_copy(w4_perm[:, a].rearrange("p t (g i) -> p g t i", i=8),
+                                  w4_raw[a][:].bitcast(U16).rearrange("p (g i t) -> p g t i", i=8, t=PACK))
+        make_rows(0, range(PACK))
         make_z(0)
         evac_and_pick(banks1, 1)
+
+        make_rows(1, range(PACK))
         make_z(1)
         table_warm = keep.tile([P, 1], F32, name="table_warm")
         nc.scalar.activation(table_warm[:], x_sb[1, PACK - 1][:, 0:1], ACT.Abs_reciprocal_sqrt, bias=1.0, scale=0.0)
 
         banks_y = new_banks()
-        for a in range(hb):
-            for i in range(8):
+        for i in range(8):
+            for a in range(hb):
                 bb, t = divmod(i, PACK)
                 c0 = bb * P
-                nc.tensor.matmul_mx(out=banks_y[i][:], lhsT=w4_perm[:, t, a, c0:c0 + P].bitcast(U8).bitcast(FP4X4), lhsT_scale=w4_sc[:, t, a, c0:c0 + P],
+                nc.tensor.matmul_mx(out=banks_y[i][:], lhsT=w4_perm[:, a, t, c0:c0 + P].bitcast(U8).bitcast(FP4X4), lhsT_scale=w4_sc[a][:, t, c0:c0 + P],
                                     rhs=z_codes[a][:].bitcast(FP8X4), rhs_scale=z_sc[a][:], start=(a == 0), stop=(a == hb - 1))
 
         out_v = out.rearrange("(c p t) m -> c p t m", p=P, t=PACK)
         for i in range(8):
             bb, t = divmod(i, PACK)
-            received = keep.tile([P, M], F32, name="received", tag=("x12", "z_rows", "zg1")[i % 3], align_bytes=64)
-            gap = keep.tile([P, M], F32, name="gap%d" % i)
+            received = keep.tile([P, M], F32, name="received%d" % i, tag=("grouped2", "zg1")[i % 2], align_bytes=64)[:]
+            gap = keep.tile([P, M], F32, name="gap%d" % i, tag="wraw0%d" % i if i < 3 else "gap%d" % i, align_bytes=64)
             inv = keep.tile([P, M], F32, name="inv%d" % i)
-            nc.vector.tensor_copy(received[:], h_sb[bb, t][:].indirect(pos2_sb[:]))
+            nc.vector.tensor_copy(received, h_sb[bb, t][:].indirect(pos2_sb[:]))
             nc.scalar.activation(inv[:], banks_y[i][:], ACT.Abs, bias=zero_bias[:])
-            nc.vector.tensor_tensor(gap[:], banks_y[i][:], received[:], ALU.subtract)
+            nc.vector.tensor_tensor(gap[:], banks_y[i][:], received, ALU.subtract)
             nc.scalar.activation(inv[:], inv[:], ACT.Abs_reciprocal_sqrt, bias=1.0)
             if i == 1:
                 nc.gpsimd.tensor_tensor(gap[:], gap[:], inv[:], ALU.mult)

@@ -43,7 +43,7 @@ def tile_list_mill_delivery_gap_kernel(tc, tab_words, tab_scales, offs, w1, pos1
         nc.vector.memset(w4_sc_raw[:].bitcast(I32), 0)
         nc.vector.memset(w4_sc[1][:].rearrange("p t n -> p (t n)").bitcast(I32), 0)
 
-        tab_sb = [keep.tile([P, T], I32, name="tab%d" % a, align_bytes=64) for a in range(ka)]
+        tab_sb = [keep.tile([P, T], I32, name="tab%d" % a, tag="tab%d" % a, align_bytes=64) for a in range(ka)]
         w_raw = {}
         for bb in range(hb):
             for a in range(ka):
@@ -98,7 +98,7 @@ def tile_list_mill_delivery_gap_kernel(tc, tab_words, tab_scales, offs, w1, pos1
         w_sc = {}
 
         def quant_w(bb, a, shares):
-            grouped = keep.tile([P, PACK * KP], BF16, name="grouped%d%d" % (bb, a), tag="grouped0%d" % a if bb == 0 and a < 2 else "grouped%d" % a, align_bytes=64)
+            grouped = keep.tile([P, PACK * KP], BF16, name="grouped%d%d" % (bb, a), tag={(0, 0): "grouped00", (0, 1): "grouped01", (1, 2): "grouped12"}.get((bb, a), "grouped%d" % a), align_bytes=64)
             dst = grouped[:].rearrange("p (t m j) -> p m j t", t=PACK, j=PACK)
             src = w_raw[bb, a][:].rearrange("p j (m t) -> p m j t", t=PACK)
             m0 = 0
@@ -109,10 +109,10 @@ def tile_list_mill_delivery_gap_kernel(tc, tab_words, tab_scales, offs, w1, pos1
                 elif engine == "vector":
                     nc.vector.tensor_copy(dst[:, cols], src[:, cols])
                 else:
-                    nc.gpsimd.tensor_scalar(dst[:, cols].rearrange("p m j t -> p t m j"), src[:, cols].rearrange("p m j t -> p t m j"), 1.0, 0.0, ALU.mult, ALU.add)
+                    nc.gpsimd.tensor_scalar(dst[:, cols].rearrange("p m j t -> p m t j"), src[:, cols].rearrange("p m j t -> p m t j"), 1.0, 0.0, ALU.mult, ALU.add)
                 m0 = m0 + width
-            w_codes[bb, a] = keep.tile([P, KP], U32, name="wc%d%d" % (bb, a), align_bytes=64)
-            w_sc[bb, a] = keep.tile([P, KP], U8, name="ws%d%d" % (bb, a), align_bytes=64)
+            w_codes[bb, a] = keep.tile([P, KP], U32, name="wc%d%d" % (bb, a), tag={(1, 2): "tab0"}.get((bb, a), "wc%d%d" % (bb, a)), align_bytes=64)
+            w_sc[bb, a] = keep.tile([P, KP], U8, name="ws%d%d" % (bb, a), tag="ws%d%d" % (bb, a), align_bytes=64)
             nc.vector.quantize_mx(out=w_codes[bb, a][:].bitcast(FP8X4), scales=w_sc[bb, a][:], in_=grouped[:])
 
         def h_pass(banks, bb, a, tiles):
@@ -138,28 +138,30 @@ def tile_list_mill_delivery_gap_kernel(tc, tab_words, tab_scales, offs, w1, pos1
                 h_sb[bb, t] = keep.tile([P, S], F32, name="h%d%d" % (bb, t))
                 for half in range(2):
                     nc.scalar.copy(h_sb[bb, t][:, half * NB:(half + 1) * NB], banks[2 * t + half][:])
-                if bb > 0 or t < PACK - 1:
+                if bb > 0:
                     pick(bb, t, "x%d%d" % (bb, t))
 
         z_codes = {}
         z_sc = {}
         z_rows = {}
+        acts = {}
 
         def make_rows(bb, tiles):
             if bb not in z_rows:
                 z_rows[bb] = keep.tile([P, PACK, M], BF16, name="z_rows%d" % bb, tag="z_rows%d" % bb, align_bytes=64)
+                acts[bb] = keep.tile([P, PACK, M], F32, name="act%d" % bb, tag=("wraw12", "tab0")[bb], align_bytes=64)
+            act = acts[bb]
             for t in tiles:
-                nc.scalar.activation(x_sb[bb, t][:], x_sb[bb, t][:], ACT.Gelu_apprx_tanh)
+                nc.scalar.activation(act[:, t, :], x_sb[bb, t][:], ACT.Gelu_apprx_tanh)
                 last = bb == hb - 1
-                (nc.vector if last else nc.gpsimd).tensor_scalar(z_rows[bb][:, t, :], x_sb[bb, t][:], gain2[:, bb, t:t + 1], b_sb[:, bb, t:t + 1], ALU.mult, ALU.add)
+                (nc.vector if last else nc.gpsimd).tensor_scalar(z_rows[bb][:, t, :], act[:, t, :], gain2[:, bb, t:t + 1], b_sb[:, bb, t:t + 1], ALU.mult, ALU.add)
 
         def make_z(bb):
-            grouped = keep.tile([P, PACK * M], BF16, name="zg%d" % bb, tag="zg%d" % bb, align_bytes=64)
+            grouped = keep.tile([P, PACK * M], BF16, name="zg%d" % bb, tag=("x10", "zg1")[bb], align_bytes=64)
             dst = grouped[:].rearrange("p (c i t) -> p c t i", i=4, t=PACK)
             src = z_rows[bb][:].rearrange("p t (c i) -> p c t i", i=4)
             if bb == 0:
-                for c0 in range(0, P, 32):
-                    nc.gpsimd.tensor_scalar(dst[:, c0:c0 + 32].rearrange("p c t i -> p c i t"), src[:, c0:c0 + 32].rearrange("p c t i -> p c i t"), 1.0, 0.0, ALU.mult, ALU.add)
+                nc.scalar.copy(dst, src)
             else:
                 nc.vector.tensor_copy(dst, src)
             z_codes[bb] = keep.tile([P, M], U32, name="zc%d" % bb, tag="zc%d" % bb, align_bytes=64)
@@ -171,7 +173,7 @@ def tile_list_mill_delivery_gap_kernel(tc, tab_words, tab_scales, offs, w1, pos1
             nc.vector.tensor_copy(v_words[a][:], tab_sb[a][:].bitcast(U32).indirect(offs_sb[:]))
 
         banks0 = new_banks()
-        shares0 = ([("scalar", 128)], [("scalar", 72), ("gpsimd", 28), ("gpsimd", 28)], [("scalar", 40), ("vector", 88)])
+        shares0 = ([("scalar", 128)], [("scalar", 64), ("vector", 64)], [("scalar", 40), ("vector", 88)])
         for a in range(ka):
             gather_words(a)
             if a == 0:
@@ -187,45 +189,52 @@ def tile_list_mill_delivery_gap_kernel(tc, tab_words, tab_scales, offs, w1, pos1
         gain2 = keep.tile([P, hb, PACK], F32, name="gain2")
         nc.gpsimd.tensor_scalar(gain2[:], gain_sb[:], 2.0, 0.0, ALU.mult, ALU.add)
         banks1 = new_banks()
-        shares1 = ([("scalar", 32), ("vector", 96)], [("gpsimd", 32)] * 4, [("scalar", 80), ("gpsimd", 24), ("gpsimd", 24)])
+        shares1 = ([("vector", 128)], [("vector", 128)], [("scalar", 128)])
         for a in range(ka):
             quant_w(1, a, shares1[a])
+            if a == 0:
+                pick(0, 0, "grouped0")
             if a == 1:
-                pick(0, PACK - 1, "grouped1")
+                pair = keep.tile([P, 2, M], F32, name="x_pair", tag="grouped1", align_bytes=64)
+                for t in (1, 2):
+                    x_sb[0, t] = pair[:, t - 1, :]
+                    nc.vector.tensor_copy(x_sb[0, t], h_sb[0, t][:].indirect(pos1_sb[:]))
         for a in range(ka):
             h_pass(banks1, 1, a, range(PACK))
-        w4_perm = keep.tile([P, hb, PACK, H // PACK], U16, name="w4_perm", tag="wraw12", align_bytes=64)
+        w4_perm = keep.tile([P, hb, PACK, H // PACK], U16, name="w4_perm", tag="grouped12", align_bytes=64)
         for a in range(hb):
             nc.vector.tensor_copy(w4_perm[:, a].rearrange("p t (g i) -> p g t i", i=8),
                                   w4_raw[a][:].bitcast(U16).rearrange("p (g i t) -> p g t i", i=8, t=PACK))
-        make_rows(0, range(PACK))
-        make_z(0)
+        pick(0, PACK - 1, "w4_raw0")
+        make_rows(0, range(PACK - 1))
         evac_and_pick(banks1, 1)
+        make_rows(0, [PACK - 1])
 
         make_rows(1, range(PACK))
         make_z(1)
+        make_z(0)
         table_warm = keep.tile([P, 1], F32, name="table_warm")
-        nc.scalar.activation(table_warm[:], x_sb[1, PACK - 1][:, 0:1], ACT.Abs_reciprocal_sqrt, bias=1.0, scale=0.0)
+        nc.scalar.activation(table_warm[:], acts[1][:, PACK - 1, 0:1], ACT.Abs_reciprocal_sqrt, bias=1.0, scale=0.0)
 
         banks_y = new_banks()
         for i in range(8):
-            for a in range(hb):
+            for a in (1, 0):
                 bb, t = divmod(i, PACK)
                 c0 = bb * P
                 nc.tensor.matmul_mx(out=banks_y[i][:], lhsT=w4_perm[:, a, t, c0:c0 + P].bitcast(U8).bitcast(FP4X4), lhsT_scale=w4_sc[a][:, t, c0:c0 + P],
-                                    rhs=z_codes[a][:].bitcast(FP8X4), rhs_scale=z_sc[a][:], start=(a == 0), stop=(a == hb - 1))
+                                    rhs=z_codes[a][:].bitcast(FP8X4), rhs_scale=z_sc[a][:], start=(a == 1), stop=(a == 0))
 
         out_v = out.rearrange("(c p t) m -> c p t m", p=P, t=PACK)
         for i in range(8):
             bb, t = divmod(i, PACK)
-            received = keep.tile([P, M], F32, name="received%d" % i, tag=("grouped2", "zg1")[i % 2], align_bytes=64)[:]
+            received = keep.tile([P, M], F32, name="received%d" % i, tag=(("zg1", "x10", "z_rows1") * 3)[i], align_bytes=64)[:]
             gap = keep.tile([P, M], F32, name="gap%d" % i, tag="wraw0%d" % i if i < 3 else "gap%d" % i, align_bytes=64)
             inv = keep.tile([P, M], F32, name="inv%d" % i)
             nc.vector.tensor_copy(received, h_sb[bb, t][:].indirect(pos2_sb[:]))
             nc.scalar.activation(inv[:], banks_y[i][:], ACT.Abs, bias=zero_bias[:])
             nc.vector.tensor_tensor(gap[:], banks_y[i][:], received, ALU.subtract)
             nc.scalar.activation(inv[:], inv[:], ACT.Abs_reciprocal_sqrt, bias=1.0)
-            if i == 1:
+            if i in (1,):
                 nc.gpsimd.tensor_tensor(gap[:], gap[:], inv[:], ALU.mult)
             else:
                 nc.scalar.activation(inv[:], inv[:], ACT.Square)

@@ -20,6 +20,7 @@ P = 128
 PACK = 4
 KP = P * PACK
 NB = 512
+RING = 3
 
 
 def tile_list_mill_delivery_gap_kernel(tc, tab_words, tab_scales, offs, w1, pos1, gain, b, w4_words, w4_scales, pos2, out):
@@ -173,7 +174,7 @@ def tile_list_mill_delivery_gap_kernel(tc, tab_words, tab_scales, offs, w1, pos1
             nc.vector.tensor_copy(v_words[a][:], tab_sb[a][:].bitcast(U32).indirect(offs_sb[:]))
 
         banks0 = new_banks()
-        shares0 = ([("scalar", 128)], [("scalar", 64), ("vector", 64)], [("scalar", 40), ("vector", 88)])
+        shares0 = ([("scalar", 128)], [("scalar", 96), ("gpsimd", 32)], [("scalar", 64), ("vector", 64)])
         for a in range(ka):
             gather_words(a)
             if a == 0:
@@ -224,10 +225,11 @@ def tile_list_mill_delivery_gap_kernel(tc, tab_words, tab_scales, offs, w1, pos1
                 nc.tensor.matmul_mx(out=banks_y[i][:], lhsT=w4_perm[:, a, t, c0:c0 + P].bitcast(U8).bitcast(FP4X4), lhsT_scale=w4_sc[a][:, t, c0:c0 + P],
                                     rhs=z_codes[a][:].bitcast(FP8X4), rhs_scale=z_sc[a][:], start=(a == 1), stop=(a == 0))
 
+        ring = keep.tile([P, RING, M], F32, name="ring", tag="zg1", align_bytes=64)
         out_v = out.rearrange("(c p t) m -> c p t m", p=P, t=PACK)
         for i in range(8):
             bb, t = divmod(i, PACK)
-            received = keep.tile([P, M], F32, name="received%d" % i, tag=(("zg1", "x10", "z_rows1") * 3)[i], align_bytes=64)[:]
+            received = ring[:, i % RING, :]
             gap = keep.tile([P, M], F32, name="gap%d" % i, tag="wraw0%d" % i if i < 3 else "gap%d" % i, align_bytes=64)
             inv = keep.tile([P, M], F32, name="inv%d" % i)
             nc.vector.tensor_copy(received, h_sb[bb, t][:].indirect(pos2_sb[:]))

@@ -80,18 +80,18 @@ def tile_list_mill_delivery_gap_kernel(tc, tab_words, tab_scales, offs, w1, pos1
         load_w(0, 0)
         load_tab(1)
         load_w(0, 1)
-        for q in range(4):
-            load_w4_scales(q)
         load_tab(2)
         nc.sync.dma_start(pos1_sb[:], pos1)
         load_w(0, 2)
-        nc.sync.dma_start(pos2_sb[:], pos2)
-        nc.sync.dma_start(gain_sb[:], gain.rearrange("(c p t) -> p c t", p=P, t=PACK))
-        nc.sync.dma_start(b_sb[:], b.rearrange("(c p t) -> p c t", p=P, t=PACK))
         for a in range(ka):
             load_w(1, a)
+        nc.sync.dma_start(gain_sb[:], gain.rearrange("(c p t) -> p c t", p=P, t=PACK))
+        nc.sync.dma_start(b_sb[:], b.rearrange("(c p t) -> p c t", p=P, t=PACK))
+        for q in range(4):
+            load_w4_scales(q)
         for a in range(hb):
             nc.sync.dma_start(w4_raw[a][:], w4_words[a].bitcast(I32))
+        nc.sync.dma_start(pos2_sb[:], pos2)
 
         v_words = {}
         v_sc = keep.tile([P, S], U8, name="v_sc", align_bytes=64)
@@ -153,9 +153,11 @@ def tile_list_mill_delivery_gap_kernel(tc, tab_words, tab_scales, offs, w1, pos1
                 acts[bb] = keep.tile([P, PACK, M], F32, name="act%d" % bb, tag=("wraw12", "tab0")[bb], align_bytes=64)
             act = acts[bb]
             for t in tiles:
-                nc.scalar.activation(act[:, t, :], x_sb[bb, t][:], ACT.Gelu_apprx_tanh)
-                last = bb == hb - 1
-                (nc.vector if last else nc.gpsimd).tensor_scalar(z_rows[bb][:, t, :], act[:, t, :], gain2[:, bb, t:t + 1], b_sb[:, bb, t:t + 1], ALU.mult, ALU.add)
+                step = M // 2 if (bb, t) == (hb - 1, PACK - 1) else M
+                for c0 in range(0, M, step):
+                    cols = slice(c0, c0 + step)
+                    nc.scalar.activation(act[:, t, cols], x_sb[bb, t][:, cols], ACT.Gelu_apprx_tanh)
+                    (nc.vector if bb == hb - 1 else nc.gpsimd).tensor_scalar(z_rows[bb][:, t, cols], act[:, t, cols], gain2[:, bb, t:t + 1], b_sb[:, bb, t:t + 1], ALU.mult, ALU.add)
 
         def make_z(bb):
             grouped = keep.tile([P, PACK * M], BF16, name="zg%d" % bb, tag=("x10", "zg1")[bb], align_bytes=64)
@@ -164,10 +166,13 @@ def tile_list_mill_delivery_gap_kernel(tc, tab_words, tab_scales, offs, w1, pos1
             if bb == 0:
                 nc.scalar.copy(dst, src)
             else:
-                nc.vector.tensor_copy(dst, src)
+                for c0 in range(0, P, P // 2):
+                    nc.vector.tensor_copy(dst[:, c0:c0 + P // 2], src[:, c0:c0 + P // 2])
             z_codes[bb] = keep.tile([P, M], U32, name="zc%d" % bb, tag="zc%d" % bb, align_bytes=64)
             z_sc[bb] = keep.tile([P, M], U8, name="zs%d" % bb, align_bytes=64)
-            nc.vector.quantize_mx(out=z_codes[bb][:].bitcast(FP8X4), scales=z_sc[bb][:], in_=grouped[:])
+            step = M // 2 if bb == hb - 1 else M
+            for c0 in range(0, M, step):
+                nc.vector.quantize_mx(out=z_codes[bb][:, c0:c0 + step].bitcast(FP8X4), scales=z_sc[bb][:, c0:c0 + step], in_=grouped[:, PACK * c0:PACK * (c0 + step)])
 
         def gather_words(a):
             v_words[a] = keep.tile([P, S], U32, name="v%d" % a, tag="grouped00" if a == 1 else "v%d" % a, align_bytes=64)
@@ -215,7 +220,7 @@ def tile_list_mill_delivery_gap_kernel(tc, tab_words, tab_scales, offs, w1, pos1
         make_z(1)
         make_z(0)
         table_warm = keep.tile([P, 1], F32, name="table_warm")
-        nc.scalar.activation(table_warm[:], acts[1][:, PACK - 1, 0:1], ACT.Abs_reciprocal_sqrt, bias=1.0, scale=0.0)
+        nc.scalar.activation(table_warm[:], acts[1][:, PACK - 1, M - 1:M], ACT.Abs_reciprocal_sqrt, bias=1.0, scale=0.0)
 
         banks_y = new_banks()
         for i in range(8):

@@ -46,12 +46,20 @@ def tile_list_mill_delivery_gap_kernel(tc, tab_words, tab_scales, offs, w1, pos1
 
         tab_sb = [keep.tile([P, T], I32, name="tab%d" % a, tag="tab%d" % a, align_bytes=64) for a in range(ka)]
         w_raw = {}
+
+        def parts(bb, a):
+            return 2 if (bb, a) == (0, 2) else 1
+
         for bb in range(hb):
             for a in range(ka):
-                w_raw[bb, a] = keep.tile([P, PACK, KP], F32, name="wraw%d%d" % (bb, a), tag="wraw%d%d" % (bb, a), align_bytes=64)
+                for s in range(parts(bb, a)):
+                    w_raw[bb, a, s] = keep.tile([P, PACK, KP // parts(bb, a)], F32, name="wraw%d%d%d" % (bb, a, s), tag="wraw%d%d" % (bb, a) + "b" * s, align_bytes=64)
 
         def load_w(bb, a):
-            nc.sync.dma_start(w_raw[bb, a][:], w1[a * KP:(a + 1) * KP, bb * KP:(bb + 1) * KP].rearrange("(p j) c -> p j c", j=PACK))
+            width = KP // parts(bb, a)
+            for s in range(parts(bb, a)):
+                c0 = bb * KP + s * width
+                nc.sync.dma_start(w_raw[bb, a, s][:], w1[a * KP:(a + 1) * KP, c0:c0 + width].rearrange("(p j) c -> p j c", j=PACK))
 
         def load_tab(a):
             nc.sync.dma_start(tab_sb[a][:], tab_words[a].rearrange("p n i -> p (n i)").bitcast(I32))
@@ -101,16 +109,17 @@ def tile_list_mill_delivery_gap_kernel(tc, tab_words, tab_scales, offs, w1, pos1
         def quant_w(bb, a, shares):
             grouped = keep.tile([P, PACK * KP], BF16, name="grouped%d%d" % (bb, a), tag={(0, 0): "grouped00", (0, 1): "grouped01", (1, 2): "grouped12"}.get((bb, a), "grouped%d" % a), align_bytes=64)
             dst = grouped[:].rearrange("p (t m j) -> p m j t", t=PACK, j=PACK)
-            src = w_raw[bb, a][:].rearrange("p j (m t) -> p m j t", t=PACK)
             m0 = 0
             for engine, width in shares:
                 cols = slice(m0, m0 + width)
+                s, s0 = divmod(m0, P // parts(bb, a))
+                src = w_raw[bb, a, s][:].rearrange("p j (m t) -> p m j t", t=PACK)[:, s0:s0 + width]
                 if engine == "scalar":
-                    nc.scalar.activation(dst[:, cols], src[:, cols], ACT.Copy)
+                    nc.scalar.copy(dst[:, cols].rearrange("p m j (u e) -> p u m j e", e=2), src.rearrange("p m j (u e) -> p u m j e", e=2))
                 elif engine == "vector":
-                    nc.vector.tensor_copy(dst[:, cols], src[:, cols])
+                    nc.vector.tensor_copy(dst[:, cols].rearrange("p m j (u e) -> p u m j e", e=2), src.rearrange("p m j (u e) -> p u m j e", e=2))
                 else:
-                    nc.gpsimd.tensor_scalar(dst[:, cols].rearrange("p m j t -> p m t j"), src[:, cols].rearrange("p m j t -> p m t j"), 1.0, 0.0, ALU.mult, ALU.add)
+                    nc.gpsimd.tensor_scalar(dst[:, cols].rearrange("p m j t -> p m t j"), src.rearrange("p m j t -> p m t j"), 1.0, 0.0, ALU.mult, ALU.add)
                 m0 = m0 + width
             w_codes[bb, a] = keep.tile([P, KP], U32, name="wc%d%d" % (bb, a), tag={(1, 2): "tab0"}.get((bb, a), "wc%d%d" % (bb, a)), align_bytes=64)
             w_sc[bb, a] = keep.tile([P, KP], U8, name="ws%d%d" % (bb, a), tag="ws%d%d" % (bb, a), align_bytes=64)
@@ -179,7 +188,7 @@ def tile_list_mill_delivery_gap_kernel(tc, tab_words, tab_scales, offs, w1, pos1
             nc.vector.tensor_copy(v_words[a][:], tab_sb[a][:].bitcast(U32).indirect(offs_sb[:]))
 
         banks0 = new_banks()
-        shares0 = ([("scalar", 128)], [("scalar", 96), ("gpsimd", 32)], [("scalar", 64), ("vector", 64)])
+        shares0 = ([("scalar", 128)], [("scalar", 96), ("gpsimd", 32)], [("scalar", 64), ("scalar", 64)])
         for a in range(ka):
             gather_words(a)
             if a == 0:

@@ -93,12 +93,12 @@ def tile_list_mill_delivery_gap_kernel(tc, tab_words, tab_scales, offs, w1, pos1
         load_w(0, 2)
         for a in range(ka):
             load_w(1, a)
+        for a in range(hb):
+            nc.sync.dma_start(w4_raw[a][:], w4_words[a].bitcast(I32))
         nc.sync.dma_start(gain_sb[:], gain.rearrange("(c p t) -> p c t", p=P, t=PACK))
         nc.sync.dma_start(b_sb[:], b.rearrange("(c p t) -> p c t", p=P, t=PACK))
         for q in range(4):
             load_w4_scales(q)
-        for a in range(hb):
-            nc.sync.dma_start(w4_raw[a][:], w4_words[a].bitcast(I32))
         nc.sync.dma_start(pos2_sb[:], pos2)
 
         v_words = {}

@@ -166,17 +166,19 @@ def tile_list_mill_delivery_gap_kernel(tc, tab_words, tab_scales, offs, w1, pos1
                 for c0 in range(0, M, step):
                     cols = slice(c0, c0 + step)
                     nc.scalar.activation(act[:, t, cols], x_sb[bb, t][:, cols], ACT.Gelu_apprx_tanh)
-                    (nc.vector if bb == hb - 1 else nc.gpsimd).tensor_scalar(z_rows[bb][:, t, cols], act[:, t, cols], gain2[:, bb, t:t + 1], b_sb[:, bb, t:t + 1], ALU.mult, ALU.add)
+                    rows = z_rows[bb][:].rearrange("p t m -> p (t m)").rearrange("p (u m e) -> p u m e", u=2, e=2)[:, t // 2, cols, t % 2]
+                    (nc.vector if bb == hb - 1 else nc.gpsimd).tensor_scalar(rows, act[:, t, cols], gain2[:, bb, t:t + 1], b_sb[:, bb, t:t + 1], ALU.mult, ALU.add)
 
         def make_z(bb):
             grouped = keep.tile([P, PACK * M], BF16, name="zg%d" % bb, tag=("x10", "zg1")[bb], align_bytes=64)
-            dst = grouped[:].rearrange("p (c i t) -> p c t i", i=4, t=PACK)
-            src = z_rows[bb][:].rearrange("p t (c i) -> p c t i", i=4)
+            word = (U32, I32)[bb]
+            dst = grouped[:].bitcast(word).rearrange("p (m u) -> p m u", u=2)
+            src = z_rows[bb][:].rearrange("p t m -> p (t m)").bitcast(word).rearrange("p (u m) -> p m u", u=2)
             if bb == 0:
                 nc.scalar.copy(dst, src)
             else:
-                for c0 in range(0, P, P // 2):
-                    nc.vector.tensor_copy(dst[:, c0:c0 + P // 2], src[:, c0:c0 + P // 2])
+                for c0 in range(0, M, M // 2):
+                    nc.vector.tensor_copy(dst[:, c0:c0 + M // 2], src[:, c0:c0 + M // 2])
             z_codes[bb] = keep.tile([P, M], U32, name="zc%d" % bb, tag="zc%d" % bb, align_bytes=64)
             z_sc[bb] = keep.tile([P, M], U8, name="zs%d" % bb, align_bytes=64)
             step = M // 2 if bb == hb - 1 else M

@@ -69,7 +69,7 @@ def tile_list_mill_delivery_gap_kernel(tc, tab_words, tab_scales, offs, w1, pos1
 
         gain_sb = keep.tile([P, hb, PACK], F32, name="gain_sb")
         b_sb = keep.tile([P, hb, PACK], F32, name="b_sb")
-        w4_raw = [keep.tile([P, H // 2], I32, name="w4_raw%d" % a, tag=("w4_raw0", "z_rows0")[a], align_bytes=64) for a in range(hb)]
+        w4_raw = [keep.tile([P, H // 2], I32, name="w4_raw%d" % a, tag="w4_raw%d" % a, align_bytes=64) for a in range(hb)]
 
         nc.sync.dma_start(offs_sb[:], offs)
         staged = keep.tile([P, T // 4], I32, name="staged", align_bytes=64)
@@ -157,8 +157,9 @@ def tile_list_mill_delivery_gap_kernel(tc, tab_words, tab_scales, offs, w1, pos1
         acts = {}
 
         def make_rows(bb, tiles):
-            if bb not in z_rows:
-                z_rows[bb] = keep.tile([P, PACK, M], BF16, name="z_rows%d" % bb, tag="z_rows%d" % bb, align_bytes=64)
+            if bb not in acts:
+                if bb > 0:
+                    z_rows[bb] = keep.tile([P, PACK * M], BF16, name="z_rows%d" % bb, tag="z_rows%d" % bb, align_bytes=64)[:]
                 acts[bb] = keep.tile([P, PACK, M], F32, name="act%d" % bb, tag=("wraw12", "tab0")[bb], align_bytes=64)
             act = acts[bb]
             for t in tiles:
@@ -166,14 +167,14 @@ def tile_list_mill_delivery_gap_kernel(tc, tab_words, tab_scales, offs, w1, pos1
                 for c0 in range(0, M, step):
                     cols = slice(c0, c0 + step)
                     nc.scalar.activation(act[:, t, cols], x_sb[bb, t][:, cols], ACT.Gelu_apprx_tanh)
-                    rows = z_rows[bb][:].rearrange("p t m -> p (t m)").rearrange("p (u m e) -> p u m e", u=2, e=2)[:, t // 2, cols, t % 2]
+                    rows = z_rows[bb].rearrange("p (u m e) -> p u m e", u=2, e=2)[:, t // 2, cols, t % 2]
                     (nc.vector if bb == hb - 1 else nc.gpsimd).tensor_scalar(rows, act[:, t, cols], gain2[:, bb, t:t + 1], b_sb[:, bb, t:t + 1], ALU.mult, ALU.add)
 
         def make_z(bb):
             grouped = keep.tile([P, PACK * M], BF16, name="zg%d" % bb, tag=("x10", "zg1")[bb], align_bytes=64)
             word = (U32, I32)[bb]
             dst = grouped[:].bitcast(word).rearrange("p (m u) -> p m u", u=2)
-            src = z_rows[bb][:].rearrange("p t m -> p (t m)").bitcast(word).rearrange("p (u m) -> p m u", u=2)
+            src = z_rows[bb].bitcast(word).rearrange("p (u m) -> p m u", u=2)
             if bb == 0:
                 nc.scalar.copy(dst, src)
             else:
@@ -218,11 +219,17 @@ def tile_list_mill_delivery_gap_kernel(tc, tab_words, tab_scales, offs, w1, pos1
                     nc.vector.tensor_copy(x_sb[0, t], h_sb[0, t][:].indirect(pos1_sb[:]))
         for a in range(ka):
             h_pass(banks1, 1, a, range(PACK))
-        w4_perm = keep.tile([P, hb, PACK, H // PACK], U16, name="w4_perm", tag="grouped12", align_bytes=64)
-        for a in range(hb):
-            nc.vector.tensor_copy(w4_perm[:, a].rearrange("p t (g i) -> p g t i", i=8),
-                                  w4_raw[a][:].bitcast(U16).rearrange("p (g i t) -> p g t i", i=8, t=PACK))
-        pick(0, PACK - 1, "w4_raw0")
+        w4_perm = {}
+
+        def reorder_w4(a, copy, tag):
+            w4_perm[a] = keep.tile([P, PACK, H // PACK], U16, name="w4_perm%d" % a, tag=tag, align_bytes=64)
+            copy(w4_perm[a][:].rearrange("p t (g i) -> p g t i", i=8), w4_raw[a][:].bitcast(U16).rearrange("p (g i t) -> p g t i", i=8, t=PACK))
+
+        reorder_w4(0, nc.vector.tensor_copy, "grouped12")
+        behind = keep.tile([P, 3 * M], F32, name="behind", tag="w4_raw0", align_bytes=64)
+        x_sb[0, PACK - 1] = behind[:, 0:M]
+        z_rows[0] = behind[:, M:3 * M].bitcast(BF16)
+        nc.vector.tensor_copy(x_sb[0, PACK - 1], h_sb[0, PACK - 1][:].indirect(pos1_sb[:]))
         make_rows(0, range(PACK - 1))
         evac_and_pick(banks1, 1)
         make_rows(0, [PACK - 1])
@@ -230,6 +237,7 @@ def tile_list_mill_delivery_gap_kernel(tc, tab_words, tab_scales, offs, w1, pos1
         make_rows(1, range(PACK))
         make_z(1)
         make_z(0)
+        reorder_w4(1, nc.scalar.copy, "x13")
         table_warm = keep.tile([P, 1], F32, name="table_warm")
         nc.scalar.activation(table_warm[:], acts[1][:, PACK - 1, M - 1:M], ACT.Abs_reciprocal_sqrt, bias=1.0, scale=0.0)
 
@@ -238,7 +246,7 @@ def tile_list_mill_delivery_gap_kernel(tc, tab_words, tab_scales, offs, w1, pos1
             for a in (1, 0):
                 bb, t = divmod(i, PACK)
                 c0 = bb * P
-                nc.tensor.matmul_mx(out=banks_y[i][:], lhsT=w4_perm[:, a, t, c0:c0 + P].bitcast(U8).bitcast(FP4X4), lhsT_scale=w4_sc[a][:, t, c0:c0 + P],
+                nc.tensor.matmul_mx(out=banks_y[i][:], lhsT=w4_perm[a][:, t, c0:c0 + P].bitcast(U8).bitcast(FP4X4), lhsT_scale=w4_sc[a][:, t, c0:c0 + P],
                                     rhs=z_codes[a][:].bitcast(FP8X4), rhs_scale=z_sc[a][:], start=(a == 1), stop=(a == 0))
 
         ring = keep.tile([P, RING, M], F32, name="ring", tag="zg1", align_bytes=64)

@@ -116,10 +116,8 @@ def tile_list_mill_delivery_gap_kernel(tc, tab_words, tab_scales, offs, w1, pos1
                 src = w_raw[bb, a, s][:].rearrange("p j (m t) -> p m j t", t=PACK)[:, s0:s0 + width]
                 if engine == "scalar":
                     nc.scalar.copy(dst[:, cols].rearrange("p m j (u e) -> p u m j e", e=2), src.rearrange("p m j (u e) -> p u m j e", e=2))
-                elif engine == "vector":
-                    nc.vector.tensor_copy(dst[:, cols].rearrange("p m j (u e) -> p u m j e", e=2), src.rearrange("p m j (u e) -> p u m j e", e=2))
                 else:
-                    nc.gpsimd.tensor_scalar(dst[:, cols].rearrange("p m j t -> p m t j"), src.rearrange("p m j t -> p m t j"), 1.0, 0.0, ALU.mult, ALU.add)
+                    nc.vector.tensor_copy(dst[:, cols].rearrange("p m j (u e) -> p u m j e", e=2), src.rearrange("p m j (u e) -> p u m j e", e=2))
                 m0 = m0 + width
             w_codes[bb, a] = keep.tile([P, KP], U32, name="wc%d%d" % (bb, a), tag={(1, 2): "tab0"}.get((bb, a), "wc%d%d" % (bb, a)), align_bytes=64)
             w_sc[bb, a] = keep.tile([P, KP], U8, name="ws%d%d" % (bb, a), tag="ws%d%d" % (bb, a), align_bytes=64)
@@ -191,7 +189,7 @@ def tile_list_mill_delivery_gap_kernel(tc, tab_words, tab_scales, offs, w1, pos1
             nc.vector.tensor_copy(v_words[a][:], tab_sb[a][:].bitcast(U32).indirect(offs_sb[:]))
 
         banks0 = new_banks()
-        shares0 = ([("scalar", 128)], [("scalar", 96), ("gpsimd", 32)], [("scalar", 64), ("scalar", 64)])
+        shares0 = ([("scalar", 128)], [("scalar", 128)], [("scalar", 64), ("scalar", 64)])
         for a in range(ka):
             gather_words(a)
             if a == 0:

@@ -39,7 +39,7 @@ def tile_list_mill_delivery_gap_kernel(tc, tab_words, tab_scales, offs, w1, pos1
         w4_sc = {1: keep.tile([P, PACK, H // PACK], U8, name="w4_sc1", align_bytes=64)}
         zero = keep.tile([P, 1], F32, name="zero")
         zero_bias = keep.tile([P, 1], F32, name="zero_bias")
-        nc.vector.memset(tab_sc[:].bitcast(I32), 0)
+        nc.gpsimd.memset(tab_sc[:].bitcast(I32), 0)
         nc.vector.memset(zero[:], 0.0)
         nc.vector.memset(w4_sc_raw[:].bitcast(I32), 0)
         nc.vector.memset(w4_sc[1][:].rearrange("p t n -> p (t n)").bitcast(I32), 0)
@@ -72,12 +72,10 @@ def tile_list_mill_delivery_gap_kernel(tc, tab_words, tab_scales, offs, w1, pos1
         w4_raw = [keep.tile([P, H // 2], I32, name="w4_raw%d" % a, tag="w4_raw%d" % a, align_bytes=64) for a in range(hb)]
 
         nc.sync.dma_start(offs_sb[:], offs)
-        staged = keep.tile([P, T // 4], I32, name="staged", align_bytes=64)
 
         def load_scale_rows(queue, q):
             rows = slice(32 * q, 32 * q + 4 * ka)
-            queue.dma_start(staged[rows, :], tab_scales[:, 4 * q:4 * q + 4, :].bitcast(I32))
-            nc.vector.tensor_copy(tab_sc[rows, :].bitcast(I32), staged[rows, :])
+            queue.dma_start(tab_sc[rows, :].bitcast(I32), tab_scales[:, 4 * q:4 * q + 4, :].bitcast(I32))
 
         load_scale_rows(nc.scalar, 0)
         load_scale_rows(nc.scalar, 1)

@@ -71,7 +71,6 @@ def tile_list_mill_delivery_gap_kernel(tc, tab_words, tab_scales, offs, w1, pos1
         b_sb = keep.tile([P, hb, PACK], F32, name="b_sb")
         w4_raw = [keep.tile([P, H // 2], I32, name="w4_raw%d" % a, tag="w4_raw%d" % a, align_bytes=64) for a in range(hb)]
 
-        nc.sync.dma_start(offs_sb[:], offs)
 
         def load_scale_rows(queue, q):
             rows = slice(32 * q, 32 * q + 4 * ka)
@@ -80,6 +79,7 @@ def tile_list_mill_delivery_gap_kernel(tc, tab_words, tab_scales, offs, w1, pos1
         load_scale_rows(nc.scalar, 0)
         load_scale_rows(nc.scalar, 1)
         load_tab(0)
+        nc.sync.dma_start(offs_sb[:], offs)
         load_scale_rows(nc.sync, 2)
         load_scale_rows(nc.sync, 3)
         nc.scalar.activation(zero_bias[:], zero[:], ACT.Gelu_apprx_tanh)
@@ -87,8 +87,8 @@ def tile_list_mill_delivery_gap_kernel(tc, tab_words, tab_scales, offs, w1, pos1
         load_tab(1)
         load_w(0, 1)
         load_tab(2)
-        nc.sync.dma_start(pos1_sb[:], pos1)
         load_w(0, 2)
+        nc.sync.dma_start(pos1_sb[:], pos1)
         for a in range(ka):
             load_w(1, a)
         for a in range(hb):
@@ -113,9 +113,9 @@ def tile_list_mill_delivery_gap_kernel(tc, tab_words, tab_scales, offs, w1, pos1
                 s, s0 = divmod(m0, P // parts(bb, a))
                 src = w_raw[bb, a, s][:].rearrange("p j (m t) -> p m j t", t=PACK)[:, s0:s0 + width]
                 if engine == "scalar":
-                    nc.scalar.copy(dst[:, cols].rearrange("p m j (u e) -> p u m j e", e=2), src.rearrange("p m j (u e) -> p u m j e", e=2))
+                    nc.scalar.copy(dst[:, cols].rearrange("p m (u e) t -> p m u t e", e=2), src.rearrange("p m (u e) t -> p m u t e", e=2))
                 else:
-                    nc.vector.tensor_copy(dst[:, cols].rearrange("p m j (u e) -> p u m j e", e=2), src.rearrange("p m j (u e) -> p u m j e", e=2))
+                    nc.vector.tensor_copy(dst[:, cols].rearrange("p m (u e) t -> p m u t e", e=2), src.rearrange("p m (u e) t -> p m u t e", e=2))
                 m0 = m0 + width
             w_codes[bb, a] = keep.tile([P, KP], U32, name="wc%d%d" % (bb, a), tag={(1, 2): "tab0"}.get((bb, a), "wc%d%d" % (bb, a)), align_bytes=64)
             w_sc[bb, a] = keep.tile([P, KP], U8, name="ws%d%d" % (bb, a), tag="ws%d%d" % (bb, a), align_bytes=64)
@@ -221,14 +221,14 @@ def tile_list_mill_delivery_gap_kernel(tc, tab_words, tab_scales, offs, w1, pos1
             w4_perm[a] = keep.tile([P, PACK, H // PACK], U16, name="w4_perm%d" % a, tag=tag, align_bytes=64)
             copy(w4_perm[a][:].rearrange("p t (g i) -> p g t i", i=8), w4_raw[a][:].bitcast(U16).rearrange("p (g i t) -> p g t i", i=8, t=PACK))
 
-        reorder_w4(0, nc.vector.tensor_copy, "grouped12")
-        behind = keep.tile([P, 3 * M], F32, name="behind", tag="w4_raw0", align_bytes=64)
-        x_sb[0, PACK - 1] = behind[:, 0:M]
-        z_rows[0] = behind[:, M:3 * M].bitcast(BF16)
+        acts[0] = keep.tile([P, PACK + 1, M], F32, name="act0", tag="wraw12", align_bytes=64)
+        x_sb[0, PACK - 1] = acts[0][:, PACK, :]
         nc.vector.tensor_copy(x_sb[0, PACK - 1], h_sb[0, PACK - 1][:].indirect(pos1_sb[:]))
-        make_rows(0, range(PACK - 1))
+        reorder_w4(0, nc.vector.tensor_copy, "grouped12")
+        z_rows[0] = keep.tile([P, PACK * M], BF16, name="z_rows0", tag="w4_raw0", align_bytes=64)[:]
+        make_rows(0, [0, 1])
         evac_and_pick(banks1, 1)
-        make_rows(0, [PACK - 1])
+        make_rows(0, [2, 3])
 
         make_rows(1, range(PACK))
         make_z(1)

@@ -48,7 +48,7 @@ def tile_list_mill_delivery_gap_kernel(tc, tab_words, tab_scales, offs, w1, pos1
         w_raw = {}
 
         def parts(bb, a):
-            return 2 if (bb, a) == (0, 2) else 1
+            return 2 if (bb, a) in ((0, 2), (1, 0)) else 1
 
         for bb in range(hb):
             for a in range(ka):
@@ -187,7 +187,7 @@ def tile_list_mill_delivery_gap_kernel(tc, tab_words, tab_scales, offs, w1, pos1
             nc.vector.tensor_copy(v_words[a][:], tab_sb[a][:].bitcast(U32).indirect(offs_sb[:]))
 
         banks0 = new_banks()
-        shares0 = ([("scalar", 128)], [("scalar", 128)], [("scalar", 64), ("scalar", 64)])
+        shares0 = ([("scalar", 128)], [("scalar", 96), ("vector", 32)], [("scalar", 64), ("scalar", 40), ("vector", 24)])
         for a in range(ka):
             gather_words(a)
             if a == 0:
@@ -203,13 +203,13 @@ def tile_list_mill_delivery_gap_kernel(tc, tab_words, tab_scales, offs, w1, pos1
         gain2 = keep.tile([P, hb, PACK], F32, name="gain2")
         nc.gpsimd.tensor_scalar(gain2[:], gain_sb[:], 2.0, 0.0, ALU.mult, ALU.add)
         banks1 = new_banks()
-        shares1 = ([("vector", 128)], [("vector", 128)], [("scalar", 128)])
+        shares1 = ([("vector", 64), ("vector", 64)], [("vector", 128)], [("scalar", 128)])
         for a in range(ka):
             quant_w(1, a, shares1[a])
             if a == 0:
-                pick(0, 0, "grouped0")
+                pick(0, 0, "wraw10b")
             if a == 1:
-                pair = keep.tile([P, 2, M], F32, name="x_pair", tag="grouped1", align_bytes=64)
+                pair = keep.tile([P, 2, M], F32, name="x_pair", tag="wraw11", align_bytes=64)
                 for t in (1, 2):
                     x_sb[0, t] = pair[:, t - 1, :]
                     nc.vector.tensor_copy(x_sb[0, t], h_sb[0, t][:].indirect(pos1_sb[:]))

from contextlib import ExitStack

import concourse.mybir as mybir

K, H, T, S, M = 1536, 1024, 2048, 1024, 512
FLOPS = 2 * K * H * S + 2 * H * H * M

F32 = mybir.dt.float32
BF16 = mybir.dt.bfloat16
I32 = mybir.dt.int32
U32 = mybir.dt.uint32
U16 = mybir.dt.uint16
U8 = mybir.dt.uint8
FP8X4 = mybir.dt.float8_e4m3fn_x4
FP4X4 = mybir.dt.float4_e2m1fn_x4
ACT = mybir.ActivationFunctionType
ALU = mybir.AluOpType

P = 128
PACK = 4
KP = P * PACK
NB = 512
RING = 3


def tile_list_mill_delivery_gap_kernel(tc, tab_words, tab_scales, offs, w1, pos1, gain, b, w4_words, w4_scales, pos2, out):
    nc = tc.nc
    ka = K // KP
    hb = H // KP
    with ExitStack() as ctx:
        keep = ctx.enter_context(tc.tile_pool(name="keep", bufs=1))
        psum = ctx.enter_context(tc.psum_pool(name="psum", bufs=1))

        offs_sb = keep.tile([P, S // 16], U16, name="offs_sb")
        pos1_sb = keep.tile([P, M // 16], U16, name="pos1_sb")
        pos2_sb = keep.tile([P, M // 16], U16, name="pos2_sb")
        tab_sc = keep.tile([P, T], U8, name="tab_sc", align_bytes=64)
        w4_sc_raw = keep.tile([P, H], U8, name="w4_sc_raw", align_bytes=64)
        w4_sc = {1: keep.tile([P, PACK, H // PACK], U8, name="w4_sc1", align_bytes=64)}
        zero = keep.tile([P, 1], F32, name="zero")
        zero_bias = keep.tile([P, 1], F32, name="zero_bias")
        nc.gpsimd.memset(tab_sc[:].bitcast(I32), 0)
        nc.vector.memset(zero[:], 0.0)
        nc.vector.memset(w4_sc_raw[:].bitcast(I32), 0)
        nc.vector.memset(w4_sc[1][:].rearrange("p t n -> p (t n)").bitcast(I32), 0)

        tab_sb = [keep.tile([P, T], I32, name="tab%d" % a, tag="tab%d" % a, align_bytes=64) for a in range(ka)]
        w_raw = {}

        def parts(bb, a):
            return 2 if (bb, a) in ((0, 2), (1, 0)) else 1

        for bb in range(hb):
            for a in range(ka):
                for s in range(parts(bb, a)):
                    w_raw[bb, a, s] = keep.tile([P, PACK, KP // parts(bb, a)], F32, name="wraw%d%d%d" % (bb, a, s), tag="wraw%d%d" % (bb, a) + "b" * s, align_bytes=64)

        def load_w(bb, a):
            width = KP // parts(bb, a)
            for s in range(parts(bb, a)):
                c0 = bb * KP + s * width
                nc.sync.dma_start(w_raw[bb, a, s][:], w1[a * KP:(a + 1) * KP, c0:c0 + width].rearrange("(p j) c -> p j c", j=PACK))

        def load_tab(a):
            nc.sync.dma_start(tab_sb[a][:], tab_words[a].rearrange("p n i -> p (n i)").bitcast(I32))

        def load_w4_scales(q):
            nc.sync.dma_start(w4_sc_raw[32 * q:32 * q + 4 * hb, :].bitcast(I32), w4_scales[:, 4 * q:4 * q + 4, :].bitcast(I32))

        gain_sb = keep.tile([P, hb, PACK], F32, name="gain_sb")
        b_sb = keep.tile([P, hb, PACK], F32, name="b_sb")
        w4_raw = [keep.tile([P, H // 2], I32, name="w4_raw%d" % a, tag="w4_raw%d" % a, align_bytes=64) for a in range(hb)]


        def load_scale_rows(queue, q):
            rows = slice(32 * q, 32 * q + 4 * ka)
            queue.dma_start(tab_sc[rows, :].bitcast(I32), tab_scales[:, 4 * q:4 * q + 4, :].bitcast(I32))

        load_scale_rows(nc.scalar, 0)
        load_scale_rows(nc.scalar, 1)
        load_tab(0)
        nc.sync.dma_start(offs_sb[:], offs)
        load_scale_rows(nc.sync, 2)
        load_scale_rows(nc.sync, 3)
        nc.scalar.activation(zero_bias[:], zero[:], ACT.Gelu_apprx_tanh)
        load_w(0, 0)
        load_tab(1)
        load_w(0, 1)
        load_tab(2)
        load_w(0, 2)
        nc.sync.dma_start(pos1_sb[:], pos1)
        for a in range(ka):
            load_w(1, a)
        for a in range(hb):
            nc.sync.dma_start(w4_raw[a][:], w4_words[a].bitcast(I32))
        nc.sync.dma_start(gain_sb[:], gain.rearrange("(c p t) -> p c t", p=P, t=PACK))
        nc.sync.dma_start(b_sb[:], b.rearrange("(c p t) -> p c t", p=P, t=PACK))
        for q in range(4):
            load_w4_scales(q)
        nc.sync.dma_start(pos2_sb[:], pos2)

        v_words = {}
        v_sc = keep.tile([P, S], U8, name="v_sc", align_bytes=64)
        w_codes = {}
        w_sc = {}

        def quant_w(bb, a, shares):
            grouped = keep.tile([P, PACK * KP], BF16, name="grouped%d%d" % (bb, a), tag={(0, 0): "grouped00", (0, 1): "grouped01", (1, 2): "grouped12"}.get((bb, a), "grouped%d" % a), align_bytes=64)
            dst = grouped[:].rearrange("p (t m j) -> p m j t", t=PACK, j=PACK)
            m0 = 0
            for engine, width in shares:
                cols = slice(m0, m0 + width)
                s, s0 = divmod(m0, P // parts(bb, a))
                src = w_raw[bb, a, s][:].rearrange("p j (m t) -> p m j t", t=PACK)[:, s0:s0 + width]
                if engine == "scalar":
                    nc.scalar.copy(dst[:, cols].rearrange("p m (u e) t -> p m u t e", e=2), src.rearrange("p m (u e) t -> p m u t e", e=2))
                else:
                    nc.vector.tensor_copy(dst[:, cols].rearrange("p m (u e) t -> p m u t e", e=2), src.rearrange("p m (u e) t -> p m u t e", e=2))
                m0 = m0 + width
            w_codes[bb, a] = keep.tile([P, KP], U32, name="wc%d%d" % (bb, a), tag={(1, 2): "tab0"}.get((bb, a), "wc%d%d" % (bb, a)), align_bytes=64)
            w_sc[bb, a] = keep.tile([P, KP], U8, name="ws%d%d" % (bb, a), tag="ws%d%d" % (bb, a), align_bytes=64)
            nc.vector.quantize_mx(out=w_codes[bb, a][:].bitcast(FP8X4), scales=w_sc[bb, a][:], in_=grouped[:])

        def h_pass(banks, bb, a, tiles):
            for t in tiles:
                for half in range(2):
                    cols = slice(t * P, (t + 1) * P)
                    ncols = slice(half * NB, (half + 1) * NB)
                    nc.tensor.matmul_mx(out=banks[2 * t + half][:], lhsT=w_codes[bb, a][:, cols].bitcast(FP8X4), lhsT_scale=w_sc[bb, a][:, cols],
                                        rhs=v_words[a][:, ncols].bitcast(FP8X4), rhs_scale=v_sc[4 * a:P, ncols], start=(a == 0), stop=(a == ka - 1))

        def new_banks():
            return [psum.tile([P, NB], F32, name="bank%d" % i) for i in range(8)]

        h_sb = {}
        x_sb = {}

        def pick(bb, t, tag):
            x_sb[bb, t] = keep.tile([P, M], F32, name="x%d%d" % (bb, t), tag=tag, align_bytes=64)
            nc.vector.tensor_copy(x_sb[bb, t][:], h_sb[bb, t][:].indirect(pos1_sb[:]))

        def evac_and_pick(banks, bb):
            for t in range(PACK):
                h_sb[bb, t] = keep.tile([P, S], F32, name="h%d%d" % (bb, t))
                for half in range(2):
                    nc.scalar.copy(h_sb[bb, t][:, half * NB:(half + 1) * NB], banks[2 * t + half][:])
                if bb > 0:
                    pick(bb, t, "x%d%d" % (bb, t))

        z_codes = {}
        z_sc = {}
        z_rows = {}
        acts = {}

        def make_rows(bb, tiles):
            if bb not in acts:
                if bb > 0:
                    z_rows[bb] = keep.tile([P, PACK * M], BF16, name="z_rows%d" % bb, tag="z_rows%d" % bb, align_bytes=64)[:]
                acts[bb] = keep.tile([P, PACK, M], F32, name="act%d" % bb, tag=("wraw12", "tab0")[bb], align_bytes=64)
            act = acts[bb]
            for t in tiles:
                step = M // 2 if (bb, t) == (hb - 1, PACK - 1) else M
                for c0 in range(0, M, step):
                    cols = slice(c0, c0 + step)
                    nc.scalar.activation(act[:, t, cols], x_sb[bb, t][:, cols], ACT.Gelu_apprx_tanh)
                    rows = z_rows[bb].rearrange("p (u m e) -> p u m e", u=2, e=2)[:, t // 2, cols, t % 2]
                    (nc.vector if bb == hb - 1 else nc.gpsimd).tensor_scalar(rows, act[:, t, cols], gain2[:, bb, t:t + 1], b_sb[:, bb, t:t + 1], ALU.mult, ALU.add)

        def make_z(bb):
            grouped = keep.tile([P, PACK * M], BF16, name="zg%d" % bb, tag=("x10", "zg1")[bb], align_bytes=64)
            word = (U32, I32)[bb]
            dst = grouped[:].bitcast(word).rearrange("p (m u) -> p m u", u=2)
            src = z_rows[bb].bitcast(word).rearrange("p (u m) -> p m u", u=2)
            if bb == 0:
                nc.scalar.copy(dst, src)
            else:
                for c0 in range(0, M, M // 2):
                    nc.vector.tensor_copy(dst[:, c0:c0 + M // 2], src[:, c0:c0 + M // 2])
            z_codes[bb] = keep.tile([P, M], U32, name="zc%d" % bb, tag="zc%d" % bb, align_bytes=64)
            z_sc[bb] = keep.tile([P, M], U8, name="zs%d" % bb, align_bytes=64)
            step = M // 2 if bb == hb - 1 else M
            for c0 in range(0, M, step):
                nc.vector.quantize_mx(out=z_codes[bb][:, c0:c0 + step].bitcast(FP8X4), scales=z_sc[bb][:, c0:c0 + step], in_=grouped[:, PACK * c0:PACK * (c0 + step)])

        def gather_words(a):
            v_words[a] = keep.tile([P, S], U32, name="v%d" % a, tag="grouped00" if a == 1 else "v%d" % a, align_bytes=64)
            nc.vector.tensor_copy(v_words[a][:], tab_sb[a][:].bitcast(U32).indirect(offs_sb[:]))

        banks0 = new_banks()
        shares0 = ([("scalar", 128)], [("scalar", 96), ("vector", 32)], [("scalar", 64), ("scalar", 40), ("vector", 24)])
        for a in range(ka):
            gather_words(a)
            if a == 0:
                nc.vector.tensor_copy(v_sc[:], tab_sc[:].indirect(offs_sb[:]))
            quant_w(0, a, shares0[a])
            h_pass(banks0, 0, a, range(PACK))

        w4_sc[0] = keep.tile([P, PACK, H // PACK], U8, name="w4_sc0", tag="grouped01", align_bytes=64)
        nc.gpsimd.tensor_copy(w4_sc[0][:].rearrange("p t (g i) -> p g t i", i=16), w4_sc_raw[:].rearrange("p (g i t) -> p g t i", i=16, t=PACK))
        for q in range(4):
            nc.sync.dma_start(w4_sc[1][32 * q:32 * q + 4].rearrange("p t n -> p (t n)").bitcast(I32), w4_sc[0][32 * q + 4:32 * q + 8].rearrange("p t n -> p (t n)").bitcast(I32))
        evac_and_pick(banks0, 0)
        gain2 = keep.tile([P, hb, PACK], F32, name="gain2")
        nc.gpsimd.tensor_scalar(gain2[:], gain_sb[:], 2.0, 0.0, ALU.mult, ALU.add)
        banks1 = new_banks()
        shares1 = ([("vector", 64), ("vector", 64)], [("vector", 128)], [("scalar", 128)])
        for a in range(ka):
            quant_w(1, a, shares1[a])
            if a == 0:
                pick(0, 0, "wraw10b")
            if a == 1:
                pair = keep.tile([P, 2, M], F32, name="x_pair", tag="wraw11", align_bytes=64)
                for t in (1, 2):
                    x_sb[0, t] = pair[:, t - 1, :]
                    nc.vector.tensor_copy(x_sb[0, t], h_sb[0, t][:].indirect(pos1_sb[:]))
        for a in range(ka):
            h_pass(banks1, 1, a, range(PACK))
        w4_perm = {}

        def reorder_w4(a, copy, tag):
            w4_perm[a] = keep.tile([P, PACK, H // PACK], U16, name="w4_perm%d" % a, tag=tag, align_bytes=64)
            copy(w4_perm[a][:].rearrange("p t (g i) -> p g t i", i=8), w4_raw[a][:].bitcast(U16).rearrange("p (g i t) -> p g t i", i=8, t=PACK))

        acts[0] = keep.tile([P, PACK + 1, M], F32, name="act0", tag="wraw12", align_bytes=64)
        x_sb[0, PACK - 1] = acts[0][:, PACK, :]
        nc.vector.tensor_copy(x_sb[0, PACK - 1], h_sb[0, PACK - 1][:].indirect(pos1_sb[:]))
        reorder_w4(0, nc.vector.tensor_copy, "grouped12")
        z_rows[0] = keep.tile([P, PACK * M], BF16, name="z_rows0", tag="w4_raw0", align_bytes=64)[:]
        make_rows(0, [0, 1])
        evac_and_pick(banks1, 1)
        make_rows(0, [2, 3])

        make_rows(1, range(PACK))
        make_z(1)
        make_z(0)
        reorder_w4(1, nc.scalar.copy, "x13")
        table_warm = keep.tile([P, 1], F32, name="table_warm")
        nc.scalar.activation(table_warm[:], acts[1][:, PACK - 1, M - 1:M], ACT.Abs_reciprocal_sqrt, bias=1.0, scale=0.0)

        banks_y = new_banks()
        for i in range(8):
            for a in (1, 0):
                bb, t = divmod(i, PACK)
                c0 = bb * P
                nc.tensor.matmul_mx(out=banks_y[i][:], lhsT=w4_perm[a][:, t, c0:c0 + P].bitcast(U8).bitcast(FP4X4), lhsT_scale=w4_sc[a][:, t, c0:c0 + P],
                                    rhs=z_codes[a][:].bitcast(FP8X4), rhs_scale=z_sc[a][:], start=(a == 1), stop=(a == 0))

        ring = keep.tile([P, RING, M], F32, name="ring", tag="zg1", align_bytes=64)
        out_v = out.rearrange("(c p t) m -> c p t m", p=P, t=PACK)
        for i in range(8):
            bb, t = divmod(i, PACK)
            received = ring[:, i % RING, :]
            gap = keep.tile([P, M], F32, name="gap%d" % i, tag="wraw0%d" % i if i < 3 else "gap%d" % i, align_bytes=64)
            inv = keep.tile([P, M], F32, name="inv%d" % i)
            nc.vector.tensor_copy(received, h_sb[bb, t][:].indirect(pos2_sb[:]))
            nc.scalar.activation(inv[:], banks_y[i][:], ACT.Abs, bias=zero_bias[:])
            nc.vector.tensor_tensor(gap[:], banks_y[i][:], received, ALU.subtract)
            nc.scalar.activation(inv[:], inv[:], ACT.Abs_reciprocal_sqrt, bias=1.0)
            if i in (1,):
                nc.gpsimd.tensor_tensor(gap[:], gap[:], inv[:], ALU.mult)
            else:
                nc.scalar.activation(inv[:], inv[:], ACT.Square)
            engine = nc.gpsimd if i < 6 else nc.vector
            engine.tensor_tensor(gap[:], gap[:], inv[:], ALU.mult)
            nc.sync.dma_start(out_v[bb, :, t, :], gap[:])
